import numpy as np, ml_dtypes
CORES = [10,34,74,98]
N = 4
import mx_ref
BF = ml_dtypes.bfloat16
def gentries(a):
    return np.ascontiguousarray(a.reshape(8, 16, -1).transpose(0, 2, 1)).reshape(8, -1)
def gtable(e):
    e = np.asarray(e); return np.ascontiguousarray(e.reshape(8, -1, 16).transpose(0, 2, 1)).reshape(128, -1).astype(np.int32)
def gcols(t, e):
    v = np.concatenate([t.reshape(8, 16, -1, 4), np.zeros((8, 16, 1, 4), BF)], axis=2)
    return np.ascontiguousarray(np.stack([v[g][:, e[g]] for g in range(8)])).reshape(128, -1)
def tile(rs):
    return np.stack(rs, axis=2).reshape(128, -1).astype(BF)
def cut(t, i, w=512):
    return t[:, w * i:w * i + w]
def pick(q, e):
    c = np.concatenate([q[0].reshape(128, -1, 4), np.zeros((128, 1, 4), np.uint8)], axis=1); s = np.concatenate([q[1], np.ones((16, 1), np.uint8)], axis=1)
    return (np.ascontiguousarray(c[:, e].reshape(128, -1)), np.ascontiguousarray(s[:, e]))
def join(*qs):
    return (np.concatenate([q[0] for q in qs], axis=1), np.concatenate([q[1] for q in qs], axis=1))
def put(q, e, v):
    c, s = q[0].reshape(128, -1, 4).copy(), q[1].copy(); c[:, e] = v[0].reshape(128, -1, 4); s[:, e] = v[1]
    return (c.reshape(128, -1), s)
def pk(c, s):
    return (np.ascontiguousarray(c), mx_ref.live(s))
def emit(q):
    return q[0], q[1]
def packed(v, rng):
    q = [mx_ref.quantize(np.ascontiguousarray(v[r])) for r in range(N)]
    return np.stack([a for a, b in q]), np.stack([mx_ref.plane(b, rng) for a, b in q])
def values_of_codes():
    e, c = np.zeros((128, 128, 4), np.float32), np.zeros((128, 2, 4), np.uint8)
    e[np.arange(128), np.arange(128), 0] = 1
    c[:127, :, 0] = np.arange(256).reshape(2, 128).T[:127]
    return mx_ref.matmul(mx_ref.quantize(e.reshape(128, 512).astype(BF)), (c.reshape(128, 8), np.full((16, 2), 127, np.uint8))).T.reshape(-1).astype(np.float64)
CODE_VALUE, SCALE_VALUE = values_of_codes(), 2.0 ** (np.arange(256) - 127.0)
def decode(q):
    return (CODE_VALUE[q[0]].reshape(16, 8, -1, 4) * SCALE_VALUE[q[1]][:, None, :, None] + 0.0).reshape(128, -1).astype(np.float32)
def f(rng, *shape):
    return mx_ref.flush((rng.standard_normal(shape, dtype=np.float32) * np.exp2(rng.integers(-2, 3, shape[:-1] + (1,)))).astype(BF))
def wide(rng, *shape, cols=0):
    v = rng.standard_normal(shape, dtype=np.float32) * np.exp2(rng.integers(-12, 13, shape)).astype(np.float32)
    if cols: v *= np.repeat(np.exp2(rng.integers(-cols, cols + 1, shape[:-2] + (1, shape[-1] // 4))) * (rng.random(shape[:-2] + (1, shape[-1] // 4)) > 0.0625), 4, axis=-1).astype(np.float32)
    return mx_ref.flush(v.astype(BF))
C, K, M, R, S = 448, 128, 2, 3, 4
def order(p):
    return np.argsort(-(p[::16] + np.float32(0.0)), axis=1, kind="stable")
def replies(o, m):
    place = np.argsort(o, axis=1)
    label = np.where(place >= C - K, 2, 0)
    when = np.zeros((8, C), int)
    for n in range(1, S + 1):
        to = np.take_along_axis(label, m, axis=1).reshape(8, M, C)
        won = (label == 0) & (to == 2).any(axis=1)
        lost = (label == 0) & (to == 1).all(axis=1)
        when[won | lost] = n
        label[won] = 1
        label[lost] = 2
    to = np.take_along_axis(label, m, axis=1).reshape(8, M, C)
    at = np.take_along_axis(when, m, axis=1).reshape(8, M, C)
    best = np.argmin(np.take_along_axis(place, m, axis=1).reshape(8, M, C), axis=1)
    k = np.where(label == 1, np.argmin(np.where(to == 2, at, S + 1), axis=1), np.where(label == 2, np.argmax(np.where(to == 1, at, -1), axis=1), best))
    t = np.take_along_axis(m.reshape(8, M, C), k[:, None], axis=1)[:, 0]
    return np.concatenate([np.where(place >= C - K, place + K, t), np.tile(C + np.arange(K), (8, 1))], axis=1)
def big(v):
    v = v.astype(np.float32)
    v[np.abs(v) < np.float32(2.0 ** -16)] = 0
    return v.astype(BF)
def numbers_of(rng):
    return {"x": big(f(rng, N, 128, 4 * C)), "u": np.array(f(rng, N, 128, 512)), "v": np.array(f(rng, N, 128, 512))}
def moves(rng):
    return np.stack([gtable(rng.integers(0, C, (8, M * C))) for r in range(N)])
def weights(rng, w):
    c, p = packed(w, rng)
    return {"wc": c, "ws": p}
def within(rng, a, b):
    w = np.array(f(rng, N, 128, 2048)).reshape(N, 8, 16, 4, 8, 16, 4)
    z = np.zeros_like(w)
    z[:, :, a:b, :, :, a:b] = w[:, :, a:b, :, :, a:b]
    return weights(rng, z.reshape(N, 128, 2048))
def signs(rng):
    return np.stack([rng.permutation(8) % 2 * 2.0 - 1.0 for r in range(N)])
def lead(rng, m, i, one, others):
    m[:, i] = rng.choice(others, (M, len(i)))
    m[rng.integers(0, M, len(i)), i] = rng.choice(one, len(i))
def game(rng, dead, rest, kind, g):
    m = rng.integers(0, C, (M, C))
    a, b, c, d, e, h = np.array_split(rng.permutation(rest), 6)
    if kind == 0:
        lead(rng, m, a, dead, np.arange(C))
        lead(rng, m, b, a, a)
        lead(rng, m, c, b, rest)
        lead(rng, m, d, c, np.concatenate([a, c]))
        lead(rng, m, e, d, np.concatenate([a, c, d, e]))
        lead(rng, m, h, h, np.concatenate([a, c, h]))
    elif kind == 1:
        lead(rng, m, rest, rest, rest)
        z = np.sort(rest[:C - 2 * K])[-2:]
        i = rng.choice(rest, 8)
        m[0, i] = z[1]
        m[1:, i] = z[0]
    elif kind == 2 and g % 2: lead(rng, m, rest, dead, np.arange(C))
    elif kind == 2: m[:] = dead[0]
    else:
        lead(rng, m, a, dead, np.arange(C))
        lead(rng, m, np.concatenate([b, c, d, e, h]), a, a)
    return m
def setup_inputs(rng):
    return {**numbers_of(rng), "mv": moves(rng), **weights(rng, f(rng, N, 128, 2048))}
def setup_inputs_ties(rng):
    d = numbers_of(rng)
    e = rng.permutation(N)
    x = d["x"].reshape(N, 8, 16, C, 4)
    for r in range(N):
        k = np.zeros(C, int) if r == e[0] else rng.permutation(C) % 3
        a = x[r][:, :8, :3].copy()
        a[:, :, 2] = 0
        x[r][:, :8] = a[:, :, k]
    x[e[1]] = 0
    u = d["u"].reshape(N, 8, 16, 128, 4)
    u[:, :, 8:, ::16] = 0
    w = np.array(f(rng, N, 128, 2048)).reshape(N, 8, 16, 4, 8, 16, 4)
    w[:, :, 8:, :, :, :8] = 0
    return {"x": x.reshape(N, 128, 4 * C), "u": u.reshape(N, 128, 512), "v": d["v"], "mv": moves(rng), **weights(rng, w.reshape(N, 128, 2048))}
def setup_inputs_near(rng):
    d = numbers_of(rng)
    x = d["x"].astype(np.float32).reshape(N, 8, 16, C, 4)
    s = np.arange(C) // 2
    g = ((s[:, None] >> np.arange(8)) & 1) * np.exp2(np.arange(8) - 23.0)
    c = np.stack([rng.permutation(8) for r in range(N)])
    z = c % 2 * 2.0 - 1.0
    x[:, :, 0] = 0
    x[:, :, 0, :, 0] = z[:, :, None]
    j = rng.integers(0, C, N)
    x[np.arange(N)[:, None], np.arange(8), 0, j[:, None], 0] = np.where(z > 0, 2.0 ** 30, np.where(c % 4 == 0, -2.0 ** 30, -1.0))
    x[:, :, 8] = g[:, :4]
    x[:, :, 9] = g[:, 4:]
    x[:, :, 10:] = rng.integers(4, 8, (N, 8, 6, C, 4)) * rng.choice([-1.0, 1.0], (N, 8, 6, C, 4)) * 2.0 ** -20
    u = d["u"].reshape(N, 128, 128, 4)
    k = np.where(rng.permutation(N) < N // 2, 2.0 ** -30, 1.0).astype(np.float32).astype(BF)
    u[:, :, ::16] = 0
    for h in range(0, 128, 16):
        u[:, h, h, 0] = k
        u[:, h + 8:h + 10, h] = k[:, None, None]
    return {"x": x.reshape(N, 128, 4 * C).astype(BF), "u": u.reshape(N, 128, 512), "v": d["v"], "mv": moves(rng), **within(rng, 1, 8)}
def setup_inputs_waves(rng):
    d = numbers_of(rng)
    o = rng.permutation(N)
    small = rng.permutation(N) < N // 2
    c = np.zeros((N, 8, C))
    m = []
    for r in range(N):
        own = []
        for g in range(8):
            e = rng.permutation(C)
            c[r, g, e[:K]] = -1
            c[r, g, e[C - K:]] = 1
            own.append(game(rng, e[:K], e[K:], o[r] % 4, g).reshape(-1))
        m.append(gtable(np.stack(own)))
    k = np.where(small, 2.0 ** -30, 1.0).astype(np.float32)
    x = d["x"].reshape(N, 8, 16, C, 4)
    x[:, :, :8] = 0
    x[:, :, 0, :, 0] = ((2.5 * np.abs(c) + 0.5 * c) * k[:, None, None]).astype(np.float32).astype(BF)
    x[:, :, 1, :, 0] = ((2.5 * np.abs(c) - 0.5 * c) * k[:, None, None]).astype(np.float32).astype(BF)
    u = d["u"].reshape(N, 128, 128, 4)
    u[:, :, ::16] = 0
    for h in range(0, 128, 16):
        u[:, h, h, 0] = k.astype(BF)
        u[:, h + 1, h, 0] = (-k).astype(BF)
    return {"x": x.reshape(N, 128, 4 * C), "u": u.reshape(N, 128, 512), "v": d["v"], "mv": np.stack(m), **within(rng, 8, 16)}
def setup_inputs_huge(rng):
    d = numbers_of(rng)
    x = 2.0 ** 29 * (0.8 + 0.2 * rng.random((N, 128, C, 4)))
    c = np.stack([rng.permutation(C) % 2 * 2.0 - 1.0 for r in range(N)])
    c[rng.permutation(N) < N // 2] = 1
    x *= c[:, None, :, None]
    u = d["u"].reshape(N, 128, 128, 4)
    a = 2.0 ** 30 * (1 - 0.25 * rng.random((N, 128, 8, 4))) * signs(rng)[:, None, :, None]
    u[:, :, ::16] = a.astype(np.float32).astype(BF)
    w = np.zeros((N, 128, 4, 128, 4), np.float32)
    i = np.arange(128)
    for b in range(4): w[:, i, b, i, b] = 4
    return {"x": x.astype(np.float32).reshape(N, 128, 4 * C).astype(BF), "u": u.reshape(N, 128, 512), "v": d["v"], "mv": moves(rng), **weights(rng, w.reshape(N, 128, 2048).astype(BF))}
def setup_inputs_spread(rng):
    d = setup_inputs(rng)
    d["x"] = big(wide(rng, N, 128, 4 * C, cols=6))
    return d
def check_inputs(d):
    b = []
    for k in ("x", "u", "v"):
        a = np.abs(d[k].astype(np.float32))
        if not (np.isfinite(a).all() and ((a == 0) | (a >= 2.0 ** -30) & (a <= 2.0 ** 30)).all()): b.append("a value of " + k)
    if ((d["mv"] < 0) | (d["mv"] >= C)).any(): b.append("an entry of mv")
    if (d["wc"] % 128 == 127).any(): b.append("a code of wc")
    none, low, high = [np.max(s) for c, s in [mx_ref.quantize(np.full((128, 16), k).astype(BF)) for k in (0.0, 2.0 ** -30, 2.0 ** 30)]]
    live = np.stack([mx_ref.live(p) for p in d["ws"]])
    if ((live != none) & ((live < low) | (live > high))).any(): b.append("a scale of ws")
    return b
def reference(x, u, v, mv, wc, ws):
    qu = [mx_ref.quantize(u[r]) for r in range(N)]
    lay = [pk(wc[r], ws[r]) for r in range(N)]
    now = [x[r] for r in range(N)]
    to = [None] * N
    for n in range(R):
        border = []
        for r in range(N):
            o = order(mx_ref.matmul(qu[r], mx_ref.quantize(now[r])))
            border.append(mx_ref.quantize(gcols(now[r], o[:, :K])))
            to[r] = replies(o, gentries(mv[r]))
        came = decode(join(*border)).astype(BF)
        for r in range(N):
            both = np.concatenate([now[r], cut(came, (r + 1) % N, 4 * K)], axis=1)
            t = to[r][:, :C]
            one = gcols(both, t).astype(np.float32)
            two = gcols(both, np.take_along_axis(to[r], t, axis=1)).astype(np.float32)
            q = mx_ref.quantize(((one + two) * np.float32(0.5)).astype(BF))
            old = now[r].astype(np.float32)
            now[r] = tile([old[:, b::4] + mx_ref.matmul(pick(lay[r], np.arange(128 * b, 128 * b + 128)), q) * np.float32(0.03125) for b in range(4)])
    y, ot = np.zeros((N, 128, C), np.float32), np.zeros((N, 8, C), np.float32)
    oc, osc = np.zeros((N, 128, 4 * C), np.uint8), np.zeros((N, 16, C), np.uint8)
    for r in range(N):
        q = mx_ref.quantize(now[r])
        y[r] = mx_ref.matmul(mx_ref.quantize(v[r]), q)
        ot[r] = to[r][:, :C]
        oc[r], osc[r] = emit(q)
    return {"y": y, "ot": ot, "oc": oc, "osc": osc}

@@ -1,0 +1,465 @@
+import numpy as np
+from concourse.mybir import dt, AluOpType, AxisListType, ActivationFunctionType
+
+C, K, ROUNDS = 448, 128, 3
+F = C + K
+H = C // 2
+NK = C // 16
+BIG = 2.0 ** 90
+OFF = 512.0
+NV = 3
+CODES, PLANE = "float8_e4m3fn_x4", "uint8"
+SMALL = ["wa", "td", "hh", "f2", "q1", "q2", "q3", "q4", "q5", "ta", "cf", "kl", "lo", "d1", "d2", "d3", "d4", "tf"]
+
+BUFFERS = {
+    "bfloat16": dict(xt=4 * C, ut=512, vt=512, ci=C, e0=K, e1=K, mask=C, dx=C, dsel=2 * C, dseg=C, dbc=2 * C, gq=512, gd=512,
+                     bd=1024, one=2 * C, et0=516, et1=516, uu=28 * C, junk=24 * C, sg=3 * C, rd=C, sp=2 * C, yb=2 * C,
+                     pw=2 * C + 16, bt=4 * K, pm=2 * C, lv=C, c2=C, b2=C + 16, ca=2 * C, r0=C, rz=C, tw=4 * F, tc=4 * C,
+                     gw=4 * F, zt=4 * C),
+    "float32": dict(mf=2 * NK, mg=2 * NK, dm=NK, pf=12, num=F, k16=NK, base=NK, ps=C, mk=C, sc=C, acc=16, a1w=NK, a2w=NK,
+                    csel=C, p128=NK, dd=2 * NK, ow=C, osel=K, t0=2 * NK, t1=2 * NK, t2=2 * NK, t3=2 * NK, otr=C, ya=H, yc=H,
+                    sm=len(SMALL) * NK),
+    "float16": dict(s1=2 * C, s2=2 * C, s3=C),
+    "int32": dict(uoi=8, mvt=2 * NK, mi=2 * NK, pi=4, aci=12, rr=NK),
+    "uint16": dict(uo=8, mo=2 * NK, mo2=2 * NK, mo3=NK, pu=NK, ou=8, tu=NK),
+    CODES: dict(xq=C, uq0=128, uq=128, vq=128, wq=512, bq=256, eq=512, cq=7 * C, zq=C, sq0=K, sq1=K, sq2=K, lq0=K, lq1=K, lq2=K),
+    PLANE: dict(xs=C, us0=128, us=128, vs=128, wp=512, bs=256, es=512, cs=7 * C, zs=C, ss0=K, ss1=K, ss2=K, ls0=K, ls1=K, ls2=K),
+}
+SCRATCH = {name: ("sbuf", [128, n], kind) for kind in BUFFERS for name, n in BUFFERS[kind].items()}
+SCRATCH.update({"p%d" % b: ("psum", [128, 512], "float32") for b in range(8)})
+
+SEMAPHORES = ["cv", "ca", "ct", "cg", "lx", "lx2", "lu", "lm", "lw", "lp", "lv", "sent", "arr0", "arr1", "arr2",
+              "o1", "o2", "o3", "o4", "o5", "o6"]
+
+A = AluOpType
+ACT = ActivationFunctionType
+
+
+def rank_program(g, core, T, topo):
+    rank = T.rank_of(core)
+    if rank is None:
+        return
+    n_ranks = len(T.cores)
+    dst = T.cores[(rank - 1) % n_ranks]
+    src_core = T.cores[(rank + 1) % n_ranks]
+    queue = {"v": g.vector, "s": g.scalar, "t": g.tensor, "g": g, "y": g.sync}
+    own = {"v": "cv", "s": "ca", "t": "ct", "g": "cg"}
+    count = {s: 0 for s in SEMAPHORES}
+    seen = {q: {s: 0 for s in SEMAPHORES} for q in queue}
+    wrote = {b: {} for b in SCRATCH}
+    read = {b: {} for b in SCRATCH}
+
+    def R(name, a=0, b=None, step=1):
+        return (name, a, SCRATCH[name][1][1] if b is None else b, step)
+
+    def ap(r):
+        if isinstance(r, tuple):
+            if len(r) == 2:
+                return ap(r[0]).indirect(ap(r[1]))
+            return T[r[0]][:, r[1]:r[2]] if r[3] == 1 else T[r[0]][:, r[1]:r[2]:r[3]]
+        return r
+
+    def raw(r):
+        return ap(r).bitcast(dt.uint8) if SCRATCH[r[0]][2] == CODES else ap(r)
+
+    def parts(rs):
+        out = []
+        for r in rs:
+            if isinstance(r, tuple):
+                out += list(r) if len(r) == 2 else [r]
+        return out
+
+    def span(r):
+        return slice(None) if SCRATCH[r[0]][0] == "psum" else slice(r[1], r[2], r[3])
+
+    def wait(q, sem, val):
+        if val > seen[q][sem]:
+            queue[q].wait_ge(T.sem[sem], val)
+            seen[q][sem] = val
+
+    def mark(table, r, sem, val):
+        if sem not in table[r[0]]:
+            table[r[0]][sem] = np.zeros(SCRATCH[r[0]][1][1], np.int64)
+        table[r[0]][sem][span(r)] = val
+
+    def before(q, reads, writes):
+        need = {}
+        for r, w in [(r, False) for r in reads] + [(r, True) for r in writes]:
+            bank = SCRATCH[r[0]][0] == "psum"
+            for table, use in ((wrote, True), (read, w or bank)):
+                for sem, v in table[r[0]].items():
+                    if not use or (bank and sem == own.get(q) and (q == "t" or table is read)):
+                        continue
+                    need[sem] = max(need.get(sem, 0), int(v[span(r)].max()))
+        for sem in need:
+            wait(q, sem, need[sem])
+
+    def op(q, make, reads, writes, sem=None, inc=1):
+        reads, writes, sem = parts(reads), parts(writes), sem or own[q]
+        before(q, reads, writes)
+        count[sem] += inc
+        make().then_inc(T.sem[sem], inc)
+        for r in reads:
+            mark(read, r, sem, count[sem])
+        for r in writes:
+            mark(wrote, r, sem, count[sem])
+
+    V, S, PE = g.vector, g.scalar, g.tensor
+
+    def copy(out, in_):
+        op("v", lambda: V.tensor_copy(ap(out), ap(in_)), [in_], [out])
+
+    def tt(out, a, b, f):
+        op("v", lambda: V.tensor_tensor(ap(out), ap(a), ap(b), f), [a, b], [out])
+
+    def ts(out, a, s1, f1, s2=None, f2=None):
+        if f2 is None:
+            op("v", lambda: V.tensor_scalar(ap(out), ap(a), ap(s1), None, f1), [a, s1], [out])
+        else:
+            op("v", lambda: V.tensor_scalar(ap(out), ap(a), ap(s1), ap(s2), f1, f2), [a, s1, s2], [out])
+
+    def scan(out, d0, d1, f0=A.add, f1=A.max):
+        op("v", lambda: V.tensor_tensor_scan(ap(out), ap(d0), ap(d1), 0.0, f0, f1), [d0, d1], [out])
+
+    def total(out, in_):
+        op("v", lambda: V.tensor_reduce(ap(out), ap(in_), AxisListType.X, A.add), [in_], [out])
+
+    def fill(out, val):
+        op("v", lambda: V.memset(ap(out), val), [], [out])
+
+    def quant(q, s, in_):
+        op("v", lambda: V.quantize_mx(ap(q), ap(s), ap(in_)), [in_], [q, s])
+
+    def act(out, in_, func=ACT.Copy, bias=None, scale=1.0, acc=None):
+        kw = {"scale": ap(scale)}
+        if bias is not None:
+            kw["bias"] = ap(bias)
+        if acc is not None:
+            kw["accum_out"] = ap(acc)
+        op("s", lambda: S.activation(ap(out), ap(in_), func, **kw), [in_, bias, scale], [out, acc])
+
+    def mm(out, wq, wsc, xq, xsc, start=True, stop=True):
+        op("t", lambda: PE.matmul_mx(ap(out), ap(wq), ap(wsc), ap(xq), ap(xsc), start, stop), [wq, wsc, xq, xsc], [out])
+
+    def iota(out, pattern, base=0, mult=0):
+        kw = {} if SCRATCH[out[0]][2] == "int32" else {"allow_small_or_imprecise_dtypes": True}
+        op("g", lambda: g.iota(ap(out), pattern, base, mult, **kw), [], [out])
+
+    def ones_where(out, n, pattern, f, base, mult):
+        op("g", lambda: g.affine_select(ap(out), ap(R("one", 0, n)), pattern, f, 0.0, base, mult), [R("one", 0, n)], [out])
+
+    def load(q, out, src, sem):
+        op(q, lambda: queue[q].dma_start(raw(out), src), [], [out], sem, 16)
+
+    def store(q, to, src, r, sem):
+        op(q, lambda: queue[q].dma_start(to, src), [r], [], sem, 16)
+
+    def col(name, j):
+        return R(name, j, j + 1)
+
+    def last(name, a=0, n=C):
+        return R(name, a + 15, a + n, 16)
+
+    def plane(name, b, a=0, e=C):
+        return R(name, F * b + a, F * b + e)
+
+    def elems(name, b, a=0, e=C):
+        return R(name, 4 * a + b, 4 * e, 4)
+
+    def block(name, b):
+        return R(name, 128 * b, 128 * b + 128)
+
+    def half(name, h, w=1):
+        return R(name, w * H * h, w * H * (h + 1))
+
+    def bank(b, n):
+        return R("p%d" % b, 0, n)
+
+    def width(s):
+        return max(128, C - 64 * s)
+
+    load("y", half("xt", 0, 4), T.x[:, 0:2 * C], "lx")
+    load("s", R("ut"), T.u[:], "lu")
+    load("y", half("xt", 1, 4), T.x[:, 2 * C:4 * C], "lx2")
+    load("s", R("mvt"), T.mv[:], "lm")
+    before("y", [R("xt")], [])
+    load("y", R("wq"), T.wc[:], "lw")
+    load("y", R("wp"), T.ws[:], "lp")
+    load("y", R("vt"), T.v[:], "lv")
+
+    iota(col("pi", 0), [[0, 1]], 0, 1)
+    iota(R("uoi"), [[16, 8]])
+    iota(R("ci"), [[0, NK], [1, 16]])
+    iota(R("k16"), [[16, NK]])
+    iota(R("gq"), [[1, 8], [0, 64]])
+    iota(R("one"), [[0, 2 * C]], 1)
+    ones_where(R("dseg"), C, [[0, NK], [1, 16]], A.is_gt, 0, 0)
+    iota(R("num"), [[1, F]])
+    iota(R("sp"), [[0, 2 * C]])
+    ones_where(R("dbc"), 2 * C, [[0, NK], [1, 32]], A.is_gt, 0, 0)
+    ones_where(R("et0"), 516, [[1, 516]], A.is_equal, -2, -4)
+    ones_where(R("et1"), 516, [[1, 516]], A.is_equal, -3, -4)
+
+    for s in range(7):
+        fill(R("uu", 4 * (s * C + C - 64 * s - 48), 4 * (s * C + width(s))), 0.0)
+    ts(col("pi", 1), col("pi", 0), 15, A.bitwise_and)
+    ts(col("pi", 2), col("pi", 0), 4, A.logical_shift_right)
+    ts(col("pi", 3), col("pi", 0), 16, A.bitwise_and)
+    copy(R("uo"), R("uoi"))
+    copy(R("pf", 0, 3), R("pi", 1, 4))
+    fill(R("rr"), 0)
+    ts(col("pf", 8), col("pf", 0), -BIG, A.mult)
+    ts(col("pf", 9), col("pf", 0), 1.0, A.add)
+    ts(col("pf", 3), col("pf", 0), 15.0, A.is_lt, OFF, A.mult)
+    act(R("mask"), R("ci"), ACT.Abs, col("pf", 8), BIG)
+    ts(R("e0"), R("ci", 0, K), col("pf", 0), A.is_equal, -4 * OFF, A.mult)
+    ts(R("e1"), R("ci", 0, K), col("pf", 9), A.is_equal, OFF, A.mult)
+    ts(R("dx"), R("ci"), 0.0, A.is_equal, -32 * BIG, A.mult)
+    tt(R("dsel", 0, K), R("e0"), R("e1"), A.add)
+    ts(col("pf", 4), col("pf", 3), col("pf", 0), A.add, -float(K + 15), A.add)
+    copy(R("dsel", K, 2 * K), R("dsel", 0, K))
+    fill(R("pw", 2 * C, 2 * C + 16), -200.0)
+    fill(R("b2", C, C + 16), 2.0)
+    ts(col("pf", 5), col("pf", 3), 128.0, A.add)
+    ts(col("pf", 6), col("pf", 3), 1.0, A.add)
+    ts(col("pf", 7), col("pf", 3), 4.0, A.add)
+    copy(R("dsel", 2 * K, C), R("dsel", 0, C - 2 * K))
+    ts(R("base"), R("k16"), col("pf", 4), A.subtract)
+    quant(R("uq0"), R("us0"), R("ut"))
+    copy(R("mo"), R("mvt"))
+    op("v", lambda: V.tensor_copy(ap(R("uq")).bitcast(dt.uint32), ap(R("uq0")).bitcast(dt.uint32).indirect(ap(R("uo")))),
+       [R("uq0"), R("uo")], [R("uq")])
+    copy(R("us"), (R("us0"), R("uo")))
+    act(R("gd"), R("gq"), ACT.Abs, col("pf", 1), -1.0)
+    act(R("bd", 0, 512), R("gd"), ACT.Relu, 1.0, -1.0)
+    for t in range(4):
+        act(R("bd", 512 + t, 1024, 4), R("bd", t, 512, 4), scale=1.0 if t < 2 else 1.0 / 512)
+    ts(R("mi"), R("mvt"), 4, A.logical_shift_right)
+    copy(R("mf"), R("mvt"))
+    ts(R("mg"), R("mi"), 16.0, A.mult, col("pf", 2), A.add)
+    tt(R("dm"), R("mf", NK, 2 * NK), R("mf", 0, NK), A.subtract)
+    tt(R("t0"), R("mg"), R("mf"), A.add)
+
+    def slot(sg, a, b):
+        s, t = sg // 4, (0, 2, 1, 3)[sg % 4]
+        return R("uu", 4 * (s * C + a) + t, 4 * (s * C + b), 4)
+
+    def pair(q):
+        a = 4 * (q // 2) * C
+        return R("uu", a + q % 2, a + 4 * (C - 32 * q), 2)
+
+    def qtile(s):
+        a, w = s * C, width(s)
+        quant(R("cq", a, a + w), R("cs", a, a + w), R("uu", 4 * a, 4 * (a + w)))
+
+    def mtile(s):
+        a, w, j = s * C, width(s), min(s, 1)
+        mm(bank(6, w), block("bq", j), block("bs", j), R("cq", a, a + w), R("cs", a, a + w), s == 0, s == 6)
+
+    def qstate(h):
+        quant(half("xq", h), half("xs", h), half("xt", h, 4))
+
+    def scores(h):
+        mm(bank(4 + h, H), R("uq"), R("us"), half("xq", h), half("xs", h))
+
+    def masked(h):
+        tt(half("mk", h), bank(4 + h, H), half("mask", h), A.subtract)
+        act(half("ps", h), bank(4 + h, H))
+
+    def moves(win, lst, k, h=None):
+        a, e = (0, NK) if h is None else (NK // 2 * h, NK // 2 * (h + 1))
+        return (win, R(lst, NK * k + a, NK * k + e))
+
+    def twin(b):
+        act(R("tc", C * b, C * b + C), plane("tw", b))
+
+    W = {w: R("sm", NK * j, NK * j + NK) for j, w in enumerate(SMALL)}
+    m0, m1 = R("mf", 0, NK), R("mf", NK, 2 * NK)
+
+    for n in range(ROUNDS):
+        first, final = n == 0, n == ROUNDS - 1
+        if first:
+            qstate(0)
+            scores(0)
+            qstate(1)
+            masked(0)
+        scores(1)
+        if first:
+            quant(R("bq"), R("bs"), R("bd"))
+        scan(half("sc", 0), half("dx", 0), half("mk", 0))
+        masked(1)
+        tt(slot(0, 0, H), bank(4, H), half("sc", 0), A.is_le)
+        scan(half("sc", 1), half("dx", 1), half("mk", 1))
+        for sg in range(1, 4):
+            a = C - 16 * sg
+            act(R("sg", (sg - 1) * C, (sg - 1) * C + a), R("ps", 0, a), ACT.Sign, col("sc", a + 15), -1.0)
+        for sg in range(1, 4):
+            a = C - 16 * sg
+            act(slot(sg, 0, a), R("sg", (sg - 1) * C, (sg - 1) * C + a), ACT.Relu, acc=col("acc", 15 - sg))
+        for sg in range(4, 28):
+            a = C - 16 * sg
+            if sg % 2:
+                ts(slot(sg, 0, a), R("ps", 0, a), col("sc", a + 15), A.is_lt, 512.0, A.mult)
+                q = sg // 2
+                if q < 14 - NV:
+                    j = 2 * C * (q - 2)
+                    act(R("junk", j, j + 2 * (C - 32 * q)), pair(q), acc=col("acc", 13 - q))
+            else:
+                ts(slot(sg, 0, a), R("ps", 0, a), col("sc", a + 15), A.is_lt)
+            if sg == 7:
+                tt(slot(0, H, C), bank(5, H), half("sc", 1), A.is_le)
+                qtile(1)
+            if sg == 12:
+                qtile(2)
+            if sg == 13:
+                qtile(0)
+                for s in range(3):
+                    mtile(s)
+            if sg in (16, 20, 24):
+                qtile(sg // 4 - 1)
+                mtile(sg // 4 - 1)
+        scan(R("rd"), R("dseg"), slot(0, 0, C), A.mult, A.add)
+        qtile(6)
+        mtile(6)
+        for q in range(14 - NV, 14):
+            total(col("acc", 13 - q), pair(q))
+        copy(R("rr", 25, 28), R("acc", 12, 15))
+        scan(R("csel"), R("dsel", 0, C), bank(6, C))
+        tt(R("a1w"), R("base"), last("rd"), A.subtract)
+        copy(R("aci"), R("acc", 0, 12))
+        tt(R("a2w"), R("a1w"), last("csel"), A.add)
+        ts(R("rr", 2, 25, 2), R("aci"), 511, A.bitwise_and)
+        ts(R("rr", 1, 25, 2), R("aci"), 9, A.logical_shift_right)
+        if first:
+            for b in range(4):
+                act(plane("tw", b), elems("xt", b), scale=32.0)
+            act(R("dsel", C, 2 * C), R("dsel", 0, C))
+        tt(R("p128"), R("a2w"), R("rr"), A.subtract)
+        sq, ss, lq, ls, arr = R("sq%d" % n), R("ss%d" % n), R("lq%d" % n), R("ls%d" % n), "arr%d" % n
+        ts(R("pu"), R("p128"), -float(K), A.add)
+        for k in range(2):
+            act(R("dd", NK * k, NK * k + NK), R("p128"), ACT.Relu, -2048.0 * (C - 0.5), 2048.0)
+        ts(R("sp", 0, 2 * C, 32), R("p128"), -320.0, A.add)
+        if not first:
+            twin(0)
+            twin(1)
+        op("v", lambda: V.tensor_copy(ap((R("ow"), R("pu"))), ap(R("num", 0, C))), [R("num", 0, C), R("pu")], [R("ow")])
+        tt(W["td"], R("p128"), R("dd", 0, NK), A.min)
+        scan(R("osel"), R("dsel", 0, K), R("ow", 0, K))
+        tt(R("t3"), R("t0"), R("dd"), A.add)
+        ts(R("ou"), last("osel", 0, K), col("pf", 3), A.subtract)
+        for b in range(4):
+            act(elems("bt", b, 0, K), (plane("tw", b), R("ou")), scale=1.0 / 32)
+        scan(R("yb"), R("dbc"), R("sp"), A.mult, A.add)
+        ts(R("mo2"), R("t3"), 2.0 * C, A.min)
+        op("v", lambda: V.transpose(ap(R("pw", 0, 2 * C)), ap(R("yb"))), [R("yb")], [R("pw", 0, 2 * C)])
+        for h in range(2):
+            act(half("pm", h), moves(R("pw"), "mo2", 0, h))
+        quant(sq, ss, R("bt"))
+        before("g", [sq, ss], [])
+        rid, pid = topo.addr(dst)[0:2]
+        for to, src in ((lq, sq), (ls, ss)):
+            g.remote_dma(raw(to), raw(src), T.sem[arr], T.sem["sent"], pid, rid, topo.mask(core, dst))
+            count["sent"] += len(topo.engines(core, dst))
+            count[arr] += len(topo.engines(src_core, core))
+        mark(wrote, lq, arr, count[arr])
+        mark(wrote, ls, arr, count[arr])
+        for h in range(2):
+            tt(half("pm", 2 + h), moves(R("pw"), "mo2", 1, h), half("pm", h), A.max)
+        ts(R("lv"), R("pm", C, 2 * C), 128.0, A.is_ge, 2.0, A.mult)
+        for h in range(2):
+            act(half("c2", h), moves(R("lv"), "mo", 0, h), scale=0.5)
+        scan(R("s1"), R("dsel"), R("pm"))
+        ts(R("t1"), last("s1", 0, 2 * C), col("pf", 5), A.is_ge, 1024.0, A.mult)
+        tt(half("b2", 0), moves(R("lv"), "mo", 1, 0), half("c2", 0), A.min)
+        tt(W["wa"], R("t1", NK, 2 * NK), m0, A.add)
+        tt(W["f2"], last("s1"), last("s1", C), A.is_equal)
+        ts(R("mo3"), W["wa"], float(C), A.min)
+        tt(half("b2", 1), moves(R("lv"), "mo", 1, 1), half("c2", 1), A.min)
+        if first:
+            twin(0)
+        for h in range(2):
+            act(half("ca", h), moves(R("b2"), "mo3", 0, h))
+        tt(W["hh"], R("t1", NK, 2 * NK), R("t1", 0, NK), A.is_gt)
+        if first:
+            for b in range(4):
+                a = 2 - 2 * (b // 2)
+                quant(block("eq", b), block("es", b), R("et%d" % (b % 2), a, a + 512))
+        for h in range(2):
+            tt(half("ca", 2 + h), moves(R("b2"), "mo", 1, h), half("ca", h), A.max)
+        if first:
+            twin(1)
+        act(R("r0"), moves(R("ca", C, 2 * C), "mo", 0), ACT.Square)
+        twin(2)
+        twin(3)
+        for b in range(4):
+            mm(bank(b, K), block("eq", b), block("es", b), lq, ls)
+        for b in range(4):
+            act(plane("tw", b, C, F), bank(b, K), scale=32.0)
+        for b in range(4):
+            act(plane("gw", b, C, F), bank(b, K), scale=64.0)
+        scan(R("s2"), R("dsel"), R("ca"))
+        ts(R("t2"), last("s2", 0, 2 * C), col("pf", 6), A.is_lt)
+        nc3, nwon = R("t2", 0, NK), R("t2", NK, 2 * NK)
+        tt(W["q1"], nc3, nwon, A.subtract)
+        tt(W["q3"], nwon, W["f2"], A.mult)
+        tt(W["cf"], nwon, R("dm"), A.mult)
+        tt(W["q2"], W["q1"], W["hh"], A.add)
+        tt(R("rz"), moves(R("ca", C, 2 * C), "mo", 1), R("r0"), A.mult)
+        tt(W["q4"], W["q2"], W["q3"], A.add)
+        scan(R("s3"), R("dsel", 0, C), R("rz"))
+        tt(W["q5"], W["q4"], R("dm"), A.mult)
+        ts(W["lo"], last("s3"), col("pf", 6), A.is_ge)
+        ts(W["kl"], last("s3"), col("pf", 7), A.is_equal)
+        tt(W["ta"], W["q5"], m0, A.add)
+        tt(W["d2"], W["cf"], W["lo"], A.mult)
+        tt(W["d1"], W["kl"], W["f2"], A.subtract)
+        tt(W["d3"], W["d2"], W["d1"], A.mult)
+        tt(W["d4"], W["d3"], W["ta"], A.add)
+        tt(W["tf"], W["d4"], W["td"], A.max)
+        copy(R("tu"), W["tf"])
+        for b in range(4):
+            tt(plane("gw", b), moves(plane("tw", b, 0, F), "tu", 0), R("tc", C * b, C * b + C), A.add)
+            if b < 3:
+                act(elems("zt", b), moves(plane("gw", b, 0, F), "tu", 0), scale=1.0 / 64)
+        ts(elems("zt", 3, 0, H), moves(plane("gw", 3, 0, F), "tu", 0, 0), 1.0 / 64, A.mult)
+        act(elems("zt", 3, H, C), moves(plane("gw", 3, 0, F), "tu", 0, 1), scale=1.0 / 64)
+        if final:
+            act(R("otr"), moves(R("num"), "tu", 0))
+            store("y", T.ot[:], T.otr[0:128:16, :], R("otr"), "o1")
+        for h in range(2):
+            quant(half("zq", h), half("zs", h), half("zt", h, 4))
+            for b in range(4):
+                mm(bank(4 - 4 * h + b, H), block("wq", b), block("wp", b), half("zq", h), half("zs", h))
+        if first:
+            quant(R("vq"), R("vs"), R("vt"))
+        for h in range(2):
+            a, e = H * h, H * h + H
+            for b in range(4):
+                if h == 1 and b == 3:
+                    qstate(0)
+                    if final:
+                        mm(bank(4, H), R("vq"), R("vs"), half("xq", 0), half("xs", 0))
+                        store("y", T.oc[:, 0:2 * C], raw(half("xq", 0)), half("xq", 0), "o2")
+                        act(R("ya"), bank(4, H))
+                        store("s", T.y[:, 0:H], ap(R("ya")), R("ya"), "o4")
+                    else:
+                        scores(0)
+                tt(plane("tw", b, a, e), plane("tw", b, a, e), bank(4 - 4 * h + b, H), A.add)
+                if h == 0 or b < 2:
+                    act(elems("xt", b, a, e), plane("tw", b, a, e), scale=1.0 / 32)
+        for b in (2, 3):
+            ts(elems("xt", b, H, C), plane("tw", b, H, C), 1.0 / 32, A.mult)
+        if not final:
+            masked(0)
+        qstate(1)
+
+    mm(bank(5, H), R("vq"), R("vs"), half("xq", 1), half("xs", 1))
+    store("y", T.oc[:, 2 * C:4 * C], raw(half("xq", 1)), half("xq", 1), "o6")
+    for k in range(4):
+        store("s", T.osc[4 * k:4 * k + 4, :], T.xs[32 * k:32 * k + 4, :], R("xs"), "o3")
+    copy(R("yc"), bank(5, H))
+    store("y", T.y[:, H:C], ap(R("yc")), R("yc"), "o5")
+    for sem in SEMAPHORES:
+        if max(seen[q][sem] for q in queue) < count[sem]:
+            wait("g", sem, count[sem])

@@ -6,30 +6,34 @@ F = C + K
 H = C // 2
 NK = C // 16
 BIG = 2.0 ** 90
-OFF = 512.0
-NV = 3
+OFF = 1024.0
+MID = 192.0
+NS = 7
+NP = (NK - 1 - NS) // 2
+WIDTH = [max(128, C - 64 * s) for s in range(7)]
+START = [sum(WIDTH[:s]) for s in range(8)]
 CODES, PLANE = "float8_e4m3fn_x4", "uint8"
-SMALL = ["wa", "td", "hh", "f2", "q1", "q2", "q3", "q4", "q5", "ta", "cf", "kl", "lo", "d1", "d2", "d3", "d4", "tf"]
+SMALL = ["wa", "td", "hh", "f2", "e1", "q", "e0", "qd", "cf", "ta", "tb", "th", "tz", "lo", "kl", "kk", "du", "tf"]
 
 BUFFERS = {
     "bfloat16": dict(xt=4 * C, ut=512, vt=512, ci=C, e0=K, e1=K, mask=C, dx=C, dsel=2 * C, dseg=C, dbc=2 * C, gq=512, gd=512,
-                     bd=1024, one=2 * C, et0=516, et1=516, uu=28 * C, junk=24 * C, sg=3 * C, rd=C, sp=2 * C, yb=2 * C,
-                     pw=2 * C + 16, bt=4 * K, pm=2 * C, lv=C, c2=C, b2=C + 16, ca=2 * C, r0=C, rz=C, tw=4 * F, tc=4 * C,
+                     bd=512, one=2 * C, et0=516, et1=516, ew=516, uu=4 * START[7], sg=3 * C, rd=C, sp=2 * C, yb=2 * C,
+                     pw=2 * C + 16, bt=4 * K, pm=2 * C, c2=C, b2=C + 16, ca=C, z3=C, r0=C, rz=C, tw=4 * F, tc=4 * C,
                      gw=4 * F, zt=4 * C),
-    "float32": dict(mf=2 * NK, mg=2 * NK, dm=NK, pf=12, num=F, k16=NK, base=NK, ps=C, mk=C, sc=C, acc=16, a1w=NK, a2w=NK,
-                    csel=C, p128=NK, dd=2 * NK, ow=C, osel=K, t0=2 * NK, t1=2 * NK, t2=2 * NK, t3=2 * NK, otr=C, ya=H, yc=H,
-                    sm=len(SMALL) * NK),
-    "float16": dict(s1=2 * C, s2=2 * C, s3=C),
-    "int32": dict(uoi=8, mvt=2 * NK, mi=2 * NK, pi=4, aci=12, rr=NK),
+    "float32": dict(mf=2 * NK, mg=2 * NK, dm=2 * NK, pf=12, num=F, k16=NK, base=NK, mk=C, sc=C, acc=NS + NP, a1w=NK, a2w=NK,
+                    junk=192 * NP, p128=NK, dd=2 * NK, ow=C, osel=K, t0=2 * NK, t1=2 * NK, t3=2 * NK, otr=C, ya=H, yc=H,
+                    csel=C, sm=len(SMALL) * NK),
+    "float16": dict(s1=2 * C, s2=C, s3=C),
+    "int32": dict(uoi=8, mvt=2 * NK, mi=2 * NK, pi=4, rr=NK + NP),
     "uint16": dict(uo=8, mo=2 * NK, mo2=2 * NK, mo3=NK, pu=NK, ou=8, tu=NK),
-    CODES: dict(xq=C, uq0=128, uq=128, vq=128, wq=512, bq=256, eq=512, cq=7 * C, zq=C, sq0=K, sq1=K, sq2=K, lq0=K, lq1=K, lq2=K),
-    PLANE: dict(xs=C, us0=128, us=128, vs=128, wp=512, bs=256, es=512, cs=7 * C, zs=C, ss0=K, ss1=K, ss2=K, ls0=K, ls1=K, ls2=K),
+    CODES: dict(xq=C, uq0=128, uq=128, vq=128, wq=512, bq=384, eq=512, cq=START[7], zq=C, sq0=K, sq1=K, sq2=K, lq0=K, lq1=K, lq2=K),
+    PLANE: dict(xs=C, us0=128, us=128, vs=128, wp=512, bs=384, es=512, cs=START[7], zs=C, ss0=K, ss1=K, ss2=K, ls0=K, ls1=K, ls2=K),
 }
 SCRATCH = {name: ("sbuf", [128, n], kind) for kind in BUFFERS for name, n in BUFFERS[kind].items()}
 SCRATCH.update({"p%d" % b: ("psum", [128, 512], "float32") for b in range(8)})
 
 SEMAPHORES = ["cv", "ca", "ct", "cg", "lx", "lx2", "lu", "lm", "lw", "lp", "lv", "sent", "arr0", "arr1", "arr2",
-              "o1", "o2", "o3", "o4", "o5", "o6"]
+              "tw0", "tw1", "tw2", "tw3", "o1", "o2", "o3", "o4", "o5", "o6"]
 
 A = AluOpType
 ACT = ActivationFunctionType
@@ -145,8 +149,8 @@ def rank_program(g, core, T, topo):
         kw = {} if SCRATCH[out[0]][2] == "int32" else {"allow_small_or_imprecise_dtypes": True}
         op("g", lambda: g.iota(ap(out), pattern, base, mult, **kw), [], [out])
 
-    def ones_where(out, n, pattern, f, base, mult):
-        op("g", lambda: g.affine_select(ap(out), ap(R("one", 0, n)), pattern, f, 0.0, base, mult), [R("one", 0, n)], [out])
+    def where(out, in_, pattern, f, other, base, mult):
+        op("g", lambda: g.affine_select(ap(out), ap(in_), pattern, f, other, base, mult), [in_], [out])
 
     def load(q, out, src, sem):
         op(q, lambda: queue[q].dma_start(raw(out), src), [], [out], sem, 16)
@@ -172,15 +176,12 @@ def rank_program(g, core, T, topo):
     def half(name, h, w=1):
         return R(name, w * H * h, w * H * (h + 1))
 
-    def bank(b, n):
-        return R("p%d" % b, 0, n)
+    def bank(b, n, a=0):
+        return R("p%d" % b, a, n)
 
-    def width(s):
-        return max(128, C - 64 * s)
-
-    load("y", half("xt", 0, 4), T.x[:, 0:2 * C], "lx")
     load("s", R("ut"), T.u[:], "lu")
-    load("y", half("xt", 1, 4), T.x[:, 2 * C:4 * C], "lx2")
+    load("y", half("xt", 1, 4), T.x[:, 2 * C:4 * C], "lx")
+    load("y", half("xt", 0, 4), T.x[:, 0:2 * C], "lx2")
     load("s", R("mvt"), T.mv[:], "lm")
     before("y", [R("xt")], [])
     load("y", R("wq"), T.wc[:], "lw")
@@ -190,88 +191,117 @@ def rank_program(g, core, T, topo):
     iota(col("pi", 0), [[0, 1]], 0, 1)
     iota(R("uoi"), [[16, 8]])
     iota(R("ci"), [[0, NK], [1, 16]])
-    iota(R("k16"), [[16, NK]])
     iota(R("gq"), [[1, 8], [0, 64]])
-    iota(R("one"), [[0, 2 * C]], 1)
-    ones_where(R("dseg"), C, [[0, NK], [1, 16]], A.is_gt, 0, 0)
+    fill(R("one"), 1.0)
+    where(R("et0"), R("one", 0, 516), [[1, 516]], A.is_equal, 0.0, -2, -4)
+    where(R("ew"), R("et0"), [[1, 516]], A.not_equal, 512.0, -3, -4)
+    iota(R("k16"), [[16, NK]])
     iota(R("num"), [[1, F]])
+    where(R("dbc"), R("one"), [[0, NK], [1, 32]], A.is_gt, 0.0, 0, 0)
     iota(R("sp"), [[0, 2 * C]])
-    ones_where(R("dbc"), 2 * C, [[0, NK], [1, 32]], A.is_gt, 0, 0)
-    ones_where(R("et0"), 516, [[1, 516]], A.is_equal, -2, -4)
-    ones_where(R("et1"), 516, [[1, 516]], A.is_equal, -3, -4)
+    where(R("et1"), R("one", 0, 516), [[1, 516]], A.is_equal, 0.0, -3, -4)
 
-    for s in range(7):
-        fill(R("uu", 4 * (s * C + C - 64 * s - 48), 4 * (s * C + width(s))), 0.0)
     ts(col("pi", 1), col("pi", 0), 15, A.bitwise_and)
     ts(col("pi", 2), col("pi", 0), 4, A.logical_shift_right)
     ts(col("pi", 3), col("pi", 0), 16, A.bitwise_and)
     copy(R("uo"), R("uoi"))
     copy(R("pf", 0, 3), R("pi", 1, 4))
-    fill(R("rr"), 0)
+    fill(R("dx"), 0.0)
     ts(col("pf", 8), col("pf", 0), -BIG, A.mult)
     ts(col("pf", 9), col("pf", 0), 1.0, A.add)
     ts(col("pf", 3), col("pf", 0), 15.0, A.is_lt, OFF, A.mult)
+    fill(R("dx", 0, C, 16), -32 * BIG)
+    for s in range(7):
+        fill(R("uu", 4 * (START[s] + C - 64 * s - 48), 4 * START[s + 1]), 0.0)
     act(R("mask"), R("ci"), ACT.Abs, col("pf", 8), BIG)
-    ts(R("e0"), R("ci", 0, K), col("pf", 0), A.is_equal, -4 * OFF, A.mult)
-    ts(R("e1"), R("ci", 0, K), col("pf", 9), A.is_equal, OFF, A.mult)
-    ts(R("dx"), R("ci"), 0.0, A.is_equal, -32 * BIG, A.mult)
-    tt(R("dsel", 0, K), R("e0"), R("e1"), A.add)
-    ts(col("pf", 4), col("pf", 3), col("pf", 0), A.add, -float(K + 15), A.add)
-    copy(R("dsel", K, 2 * K), R("dsel", 0, K))
-    fill(R("pw", 2 * C, 2 * C + 16), -200.0)
-    fill(R("b2", C, C + 16), 2.0)
-    ts(col("pf", 5), col("pf", 3), 128.0, A.add)
-    ts(col("pf", 6), col("pf", 3), 1.0, A.add)
-    ts(col("pf", 7), col("pf", 3), 4.0, A.add)
-    copy(R("dsel", 2 * K, C), R("dsel", 0, C - 2 * K))
-    ts(R("base"), R("k16"), col("pf", 4), A.subtract)
+    act(R("gd"), R("gq"), ACT.Abs, col("pf", 1), -1.0)
+    act(R("bd"), R("gd"), ACT.Relu, 1.0, -1.0)
     quant(R("uq0"), R("us0"), R("ut"))
-    copy(R("mo"), R("mvt"))
     op("v", lambda: V.tensor_copy(ap(R("uq")).bitcast(dt.uint32), ap(R("uq0")).bitcast(dt.uint32).indirect(ap(R("uo")))),
        [R("uq0"), R("uo")], [R("uq")])
-    copy(R("us"), (R("us0"), R("uo")))
-    act(R("gd"), R("gq"), ACT.Abs, col("pf", 1), -1.0)
-    act(R("bd", 0, 512), R("gd"), ACT.Relu, 1.0, -1.0)
-    for t in range(4):
-        act(R("bd", 512 + t, 1024, 4), R("bd", t, 512, 4), scale=1.0 if t < 2 else 1.0 / 512)
-    ts(R("mi"), R("mvt"), 4, A.logical_shift_right)
-    copy(R("mf"), R("mvt"))
-    ts(R("mg"), R("mi"), 16.0, A.mult, col("pf", 2), A.add)
-    tt(R("dm"), R("mf", NK, 2 * NK), R("mf", 0, NK), A.subtract)
-    tt(R("t0"), R("mg"), R("mf"), A.add)
+    op("s", lambda: S.activation(ap(R("us")), ap((R("us0"), R("uo"))), ACT.Copy), [R("us0"), R("uo")], [R("us")])
+    ts(R("e0"), R("ci", 0, K), col("pf", 0), A.is_equal, -4 * OFF, A.mult)
+    ts(R("e1"), R("ci", 0, K), col("pf", 9), A.is_equal, OFF, A.mult)
+    act(R("dseg"), R("ci"), ACT.Sign)
+    for j, c in ((5, 128.0), (6, 1.0), (7, 35.5), (10, 4096.0)):
+        act(col("pf", j), col("pf", 3), ACT.Identity, c)
+
+    def later_constants(j):
+        if j == 0:
+            tt(R("dsel", 0, K), R("e0"), R("e1"), A.add)
+            ts(col("pf", 4), col("pf", 3), col("pf", 0), A.add, -(K + 15.0), A.add)
+            copy(R("dsel", K, 2 * K), R("dsel", 0, K))
+            fill(col("rr", 0), 0)
+            copy(R("dsel", 2 * K, C), R("dsel", 0, C - 2 * K))
+        else:
+            ts(R("base"), R("k16"), col("pf", 4), A.subtract)
+            fill(R("pw", 2 * C, 2 * C + 16), -200.0)
+            fill(R("b2", C, C + 16), -8.0)
+            copy(R("mo"), R("mvt"))
+            ts(R("mi"), R("mvt"), 4, A.logical_shift_right)
+            copy(R("mf"), R("mvt"))
+            ts(R("mg"), R("mi"), 16.0, A.mult, col("pf", 2), A.add)
+            tt(R("dm", 0, NK), R("mf", NK, 2 * NK), R("mf", 0, NK), A.subtract)
+            tt(R("t0"), R("mg"), R("mf"), A.add)
 
     def slot(sg, a, b):
-        s, t = sg // 4, (0, 2, 1, 3)[sg % 4]
-        return R("uu", 4 * (s * C + a) + t, 4 * (s * C + b), 4)
+        at = START[sg // 4]
+        return R("uu", 4 * (at + a) + sg % 4, 4 * (at + b), 4)
 
-    def pair(q):
-        a = 4 * (q // 2) * C
-        return R("uu", a + q % 2, a + 4 * (C - 32 * q), 2)
-
-    def qtile(s):
-        a, w = s * C, width(s)
+    def qtiles(s, w):
+        a = START[s]
         quant(R("cq", a, a + w), R("cs", a, a + w), R("uu", 4 * a, 4 * (a + w)))
 
-    def mtile(s):
-        a, w, j = s * C, width(s), min(s, 1)
-        mm(bank(6, w), block("bq", j), block("bs", j), R("cq", a, a + w), R("cs", a, a + w), s == 0, s == 6)
+    def mcount(b, j, a, w, start=True, stop=True):
+        mm(bank(b, w), block("bq", j), block("bs", j), R("cq", a, a + w), R("cs", a, a + w), start, stop)
+
+    def mtile(s, start=False, stop=False):
+        mcount(3, 0, START[s], WIDTH[s], start, stop)
+
+    def mpair(q, b, runs):
+        s = q // 2
+        w = WIDTH[s] // runs
+        for j in range(runs):
+            mcount(b, 1 + q % 2, START[s] + w * j, w, j == 0, j == runs - 1)
+
+    def spair(q, who):
+        b, a, w = (q, 0, WIDTH[q // 2] // 2) if q < 8 else (q % 2, START[q // 2] - START[4], C - 32 * q)
+        to = col("acc", NS + 13 - q)
+        if who == "s":
+            act(R("junk", 192 * (13 - q), 192 * (13 - q) + w), bank(b, a + w, a), acc=to)
+        else:
+            total(to, bank(b, a + w, a))
+
+    def sign(sg):
+        a = C - 16 * sg
+        act(R("sg", sg % 3 * C, sg % 3 * C + a), bank(2, a), ACT.Sign, col("sc", a + 15), -1.0)
+
+    def relu(sg):
+        a = C - 16 * sg
+        act(slot(sg, 0, a), R("sg", sg % 3 * C, sg % 3 * C + a), ACT.Relu, acc=col("acc", NS - sg))
+
+    def rows(first, end):
+        for sg in range(first, end):
+            a = C - 16 * sg
+            ts(slot(sg, 0, a), bank(1, a), col("sc", a + 15), A.is_lt)
 
     def qstate(h):
         quant(half("xq", h), half("xs", h), half("xt", h, 4))
 
-    def scores(h):
-        mm(bank(4 + h, H), R("uq"), R("us"), half("xq", h), half("xs", h))
-
-    def masked(h):
-        tt(half("mk", h), bank(4 + h, H), half("mask", h), A.subtract)
-        act(half("ps", h), bank(4 + h, H))
+    def upper_scores():
+        mm(bank(0, H), R("uq"), R("us"), half("xq", 1), half("xs", 1))
 
     def moves(win, lst, k, h=None):
         a, e = (0, NK) if h is None else (NK // 2 * h, NK // 2 * (h + 1))
         return (win, R(lst, NK * k + a, NK * k + e))
 
     def twin(b):
-        act(R("tc", C * b, C * b + C), plane("tw", b))
+        to, src = R("tc", C * b, C * b + C), plane("tw", b)
+        op("y", lambda: g.sync.dma_start(ap(to), ap(src)), [src], [to], "tw%d" % b, 16)
+
+    def two(w):
+        j = SMALL.index(w)
+        return R("sm", NK * j, NK * j + 2 * NK)
 
     W = {w: R("sm", NK * j, NK * j + NK) for j, w in enumerate(SMALL)}
     m0, m1 = R("mf", 0, NK), R("mf", NK, 2 * NK)
@@ -279,70 +309,85 @@ def rank_program(g, core, T, topo):
     for n in range(ROUNDS):
         first, final = n == 0, n == ROUNDS - 1
         if first:
-            qstate(0)
-            scores(0)
             qstate(1)
-            masked(0)
-        scores(1)
+            upper_scores()
+            later_constants(0)
+            qstate(0)
+        for b in (2, 1):
+            mm(bank(b, C), R("uq"), R("us"), R("xq"), R("xs"))
+        tt(half("mk", 1), bank(0, H), half("mask", 1), A.subtract)
         if first:
-            quant(R("bq"), R("bs"), R("bd"))
-        scan(half("sc", 0), half("dx", 0), half("mk", 0))
-        masked(1)
-        tt(slot(0, 0, H), bank(4, H), half("sc", 0), A.is_le)
+            quant(block("bq", 0), block("bs", 0), R("bd"))
         scan(half("sc", 1), half("dx", 1), half("mk", 1))
-        for sg in range(1, 4):
-            a = C - 16 * sg
-            act(R("sg", (sg - 1) * C, (sg - 1) * C + a), R("ps", 0, a), ACT.Sign, col("sc", a + 15), -1.0)
-        for sg in range(1, 4):
-            a = C - 16 * sg
-            act(slot(sg, 0, a), R("sg", (sg - 1) * C, (sg - 1) * C + a), ACT.Relu, acc=col("acc", 15 - sg))
-        for sg in range(4, 28):
-            a = C - 16 * sg
-            if sg % 2:
-                ts(slot(sg, 0, a), R("ps", 0, a), col("sc", a + 15), A.is_lt, 512.0, A.mult)
-                q = sg // 2
-                if q < 14 - NV:
-                    j = 2 * C * (q - 2)
-                    act(R("junk", j, j + 2 * (C - 32 * q)), pair(q), acc=col("acc", 13 - q))
-            else:
-                ts(slot(sg, 0, a), R("ps", 0, a), col("sc", a + 15), A.is_lt)
-            if sg == 7:
-                tt(slot(0, H, C), bank(5, H), half("sc", 1), A.is_le)
-                qtile(1)
-            if sg == 12:
-                qtile(2)
-            if sg == 13:
-                qtile(0)
-                for s in range(3):
-                    mtile(s)
-            if sg in (16, 20, 24):
-                qtile(sg // 4 - 1)
-                mtile(sg // 4 - 1)
+        tt(half("mk", 0), bank(1, H), half("mask", 0), A.subtract)
+        sign(1)
+        sign(2)
+        relu(1)
+        sign(3)
+        relu(2)
+        sign(4)
+        relu(3)
+        rows(8, 10)
+        scan(half("sc", 0), half("dx", 0), half("mk", 0))
+        rows(10, 12)
+        if first:
+            for j in range(2):
+                quant(block("bq", 1 + j), block("bs", 1 + j), R("ew", 2 - 2 * j, 514 - 2 * j))
+        qtiles(2, WIDTH[2])
+        mpair(4, 4, 2)
+        mpair(5, 5, 2)
+        rows(12, 16)
+        qtiles(3, WIDTH[3])
+        mpair(6, 6, 2)
+        mpair(7, 7, 2)
+        sign(5)
+        relu(4)
+        tt(slot(0, 0, C), bank(1, C), R("sc"), A.is_le)
+        rows(16, 18)
+        qtiles(0, C)
+        for s in (0, 2, 3):
+            mtile(s, start=s == 0)
+        rows(18, 28)
+        qtiles(4, 448 if first else 384)
+        for j in range(2):
+            mcount(j, 1 + j, START[4], 384)
+        for s in (4, 5, 6):
+            mtile(s)
+        sign(6)
+        relu(5)
+        sign(7)
+        relu(6)
+        relu(7)
         scan(R("rd"), R("dseg"), slot(0, 0, C), A.mult, A.add)
-        qtile(6)
-        mtile(6)
-        for q in range(14 - NV, 14):
-            total(col("acc", 13 - q), pair(q))
-        copy(R("rr", 25, 28), R("acc", 12, 15))
-        scan(R("csel"), R("dsel", 0, C), bank(6, C))
+        if first:
+            later_constants(1)
+        qtiles(1, WIDTH[1])
+        mtile(1, stop=True)
+        for q in (4, 5, 6, 7, 8):
+            spair(q, "s")
+        for q in (13, 11, 9):
+            spair(q, "v")
         tt(R("a1w"), R("base"), last("rd"), A.subtract)
-        copy(R("aci"), R("acc", 0, 12))
+        scan(R("csel"), R("dsel", 0, C), bank(3, C))
+        for q in (12, 10):
+            spair(q, "v")
         tt(R("a2w"), R("a1w"), last("csel"), A.add)
-        ts(R("rr", 2, 25, 2), R("aci"), 511, A.bitwise_and)
-        ts(R("rr", 1, 25, 2), R("aci"), 9, A.logical_shift_right)
+        copy(R("rr", NK - NS, NK + NP), R("acc"))
+        ts(R("rr", 2, 2 * NP + 1, 2), R("rr", NK, NK + NP), 511, A.bitwise_and)
+        ts(R("rr", 1, 2 * NP + 1, 2), R("rr", NK, NK + NP), 9, A.logical_shift_right)
         if first:
             for b in range(4):
                 act(plane("tw", b), elems("xt", b), scale=32.0)
+                twin(b)
             act(R("dsel", C, 2 * C), R("dsel", 0, C))
-        tt(R("p128"), R("a2w"), R("rr"), A.subtract)
+            act(R("dm", NK, 2 * NK), R("dm", 0, NK))
+        tt(R("p128"), R("a2w"), R("rr", 0, NK), A.subtract)
         sq, ss, lq, ls, arr = R("sq%d" % n), R("ss%d" % n), R("lq%d" % n), R("ls%d" % n), "arr%d" % n
         ts(R("pu"), R("p128"), -float(K), A.add)
         for k in range(2):
             act(R("dd", NK * k, NK * k + NK), R("p128"), ACT.Relu, -2048.0 * (C - 0.5), 2048.0)
-        ts(R("sp", 0, 2 * C, 32), R("p128"), -320.0, A.add)
-        if not first:
-            twin(0)
-            twin(1)
+        act(W["tz"], R("dd", 0, NK), ACT.Identity, col("pf", 3))
+        ts(R("sp", 0, 2 * C, 32), R("p128"), -(K + MID), A.add, 128.0, A.min)
         op("v", lambda: V.tensor_copy(ap((R("ow"), R("pu"))), ap(R("num", 0, C))), [R("num", 0, C), R("pu")], [R("ow")])
         tt(W["td"], R("p128"), R("dd", 0, NK), A.min)
         scan(R("osel"), R("dsel", 0, K), R("ow", 0, K))
@@ -364,102 +409,94 @@ def rank_program(g, core, T, topo):
             count[arr] += len(topo.engines(src_core, core))
         mark(wrote, lq, arr, count[arr])
         mark(wrote, ls, arr, count[arr])
+        won = R("pm", C, 2 * C)
         for h in range(2):
             tt(half("pm", 2 + h), moves(R("pw"), "mo2", 1, h), half("pm", h), A.max)
-        ts(R("lv"), R("pm", C, 2 * C), 128.0, A.is_ge, 2.0, A.mult)
         for h in range(2):
-            act(half("c2", h), moves(R("lv"), "mo", 0, h), scale=0.5)
+            act(half("c2", h), moves(won, "mo", 0, h), ACT.Identity, 639.5, -4.0)
         scan(R("s1"), R("dsel"), R("pm"))
         ts(R("t1"), last("s1", 0, 2 * C), col("pf", 5), A.is_ge, 1024.0, A.mult)
-        tt(half("b2", 0), moves(R("lv"), "mo", 1, 0), half("c2", 0), A.min)
-        tt(W["wa"], R("t1", NK, 2 * NK), m0, A.add)
-        tt(W["f2"], last("s1"), last("s1", C), A.is_equal)
-        ts(R("mo3"), W["wa"], float(C), A.min)
-        tt(half("b2", 1), moves(R("lv"), "mo", 1, 1), half("c2", 1), A.min)
-        if first:
-            twin(0)
+        tt(half("b2", 0), moves(won, "mo", 1, 0), half("c2", 0), A.is_ge)
+        tt(W["wa"], R("t1", NK, 2 * NK), m1, A.add)
+        tt(half("b2", 1), moves(won, "mo", 1, 1), half("c2", 1), A.is_ge)
         for h in range(2):
-            act(half("ca", h), moves(R("b2"), "mo3", 0, h))
+            act(half("ca", h), moves(R("b2"), "mo", 0, h), scale=2.0)
+        ts(R("mo3"), W["wa"], float(C), A.min)
+        tt(W["f2"], last("s1"), last("s1", C), A.is_equal)
         tt(W["hh"], R("t1", NK, 2 * NK), R("t1", 0, NK), A.is_gt)
+        ts(W["th"], W["f2"], -4096.0, A.mult, col("pf", 10), A.add)
         if first:
             for b in range(4):
                 a = 2 - 2 * (b // 2)
                 quant(block("eq", b), block("es", b), R("et%d" % (b % 2), a, a + 512))
         for h in range(2):
-            tt(half("ca", 2 + h), moves(R("b2"), "mo", 1, h), half("ca", h), A.max)
-        if first:
-            twin(1)
-        act(R("r0"), moves(R("ca", C, 2 * C), "mo", 0), ACT.Square)
-        twin(2)
-        twin(3)
+            tt(half("z3", h), moves(R("b2"), "mo3", 0, h), half("ca", h), A.add)
+        for h in range(2):
+            act(half("r0", h), moves(R("z3"), "mo", 0, h), ACT.Square)
         for b in range(4):
             mm(bank(b, K), block("eq", b), block("es", b), lq, ls)
         for b in range(4):
             act(plane("tw", b, C, F), bank(b, K), scale=32.0)
         for b in range(4):
             act(plane("gw", b, C, F), bank(b, K), scale=64.0)
-        scan(R("s2"), R("dsel"), R("ca"))
-        ts(R("t2"), last("s2", 0, 2 * C), col("pf", 6), A.is_lt)
-        nc3, nwon = R("t2", 0, NK), R("t2", NK, 2 * NK)
-        tt(W["q1"], nc3, nwon, A.subtract)
-        tt(W["q3"], nwon, W["f2"], A.mult)
-        tt(W["cf"], nwon, R("dm"), A.mult)
-        tt(W["q2"], W["q1"], W["hh"], A.add)
-        tt(R("rz"), moves(R("ca", C, 2 * C), "mo", 1), R("r0"), A.mult)
-        tt(W["q4"], W["q2"], W["q3"], A.add)
+        scan(R("s2"), R("dsel", 0, C), R("z3"))
+        ts(W["e1"], last("s2"), col("pf", 6), A.is_equal)
+        tt(W["e0"], last("s2"), W["tz"], A.is_equal)
+        tt(half("rz", 0), moves(R("z3"), "mo", 1, 0), half("r0", 0), A.mult)
+        tt(W["q"], W["e1"], W["hh"], A.add)
+        tt(half("rz", 1), moves(R("z3"), "mo", 1, 1), half("r0", 1), A.mult)
+        tt(two("qd"), two("q"), R("dm"), A.mult)
         scan(R("s3"), R("dsel", 0, C), R("rz"))
-        tt(W["q5"], W["q4"], R("dm"), A.mult)
-        ts(W["lo"], last("s3"), col("pf", 6), A.is_ge)
-        ts(W["kl"], last("s3"), col("pf", 7), A.is_equal)
-        tt(W["ta"], W["q5"], m0, A.add)
-        tt(W["d2"], W["cf"], W["lo"], A.mult)
-        tt(W["d1"], W["kl"], W["f2"], A.subtract)
-        tt(W["d3"], W["d2"], W["d1"], A.mult)
-        tt(W["d4"], W["d3"], W["ta"], A.add)
-        tt(W["tf"], W["d4"], W["td"], A.max)
+        tt(W["ta"], W["qd"], m0, A.add)
+        tt(W["lo"], last("s3"), W["th"], A.is_equal)
+        ts(W["kl"], last("s3"), col("pf", 7), A.is_ge)
+        tt(W["tb"], W["ta"], W["td"], A.max)
+        tt(W["kk"], W["lo"], W["kl"], A.add)
+        tt(W["du"], W["kk"], W["cf"], A.mult)
+        tt(W["tf"], W["du"], W["tb"], A.add)
         copy(R("tu"), W["tf"])
         for b in range(4):
             tt(plane("gw", b), moves(plane("tw", b, 0, F), "tu", 0), R("tc", C * b, C * b + C), A.add)
             if b < 3:
                 act(elems("zt", b), moves(plane("gw", b, 0, F), "tu", 0), scale=1.0 / 64)
-        ts(elems("zt", 3, 0, H), moves(plane("gw", 3, 0, F), "tu", 0, 0), 1.0 / 64, A.mult)
-        act(elems("zt", 3, H, C), moves(plane("gw", 3, 0, F), "tu", 0, 1), scale=1.0 / 64)
+        ts(elems("zt", 3, H, C), moves(plane("gw", 3, 0, F), "tu", 0, 1), 1.0 / 64, A.mult)
+        act(elems("zt", 3, 0, H), moves(plane("gw", 3, 0, F), "tu", 0, 0), scale=1.0 / 64)
         if final:
             act(R("otr"), moves(R("num"), "tu", 0))
             store("y", T.ot[:], T.otr[0:128:16, :], R("otr"), "o1")
-        for h in range(2):
+        for h in (1, 0):
             quant(half("zq", h), half("zs", h), half("zt", h, 4))
             for b in range(4):
                 mm(bank(4 - 4 * h + b, H), block("wq", b), block("wp", b), half("zq", h), half("zs", h))
         if first:
             quant(R("vq"), R("vs"), R("vt"))
-        for h in range(2):
+        for h in (1, 0):
             a, e = H * h, H * h + H
             for b in range(4):
-                if h == 1 and b == 3:
-                    qstate(0)
+                if h == 0 and b == 3:
+                    qstate(1)
                     if final:
-                        mm(bank(4, H), R("vq"), R("vs"), half("xq", 0), half("xs", 0))
-                        store("y", T.oc[:, 0:2 * C], raw(half("xq", 0)), half("xq", 0), "o2")
-                        act(R("ya"), bank(4, H))
-                        store("s", T.y[:, 0:H], ap(R("ya")), R("ya"), "o4")
+                        mm(bank(0, H), R("vq"), R("vs"), half("xq", 1), half("xs", 1))
+                        store("y", T.oc[:, 2 * C:4 * C], raw(half("xq", 1)), half("xq", 1), "o2")
+                        act(R("ya"), bank(0, H))
+                        store("s", T.y[:, H:C], ap(R("ya")), R("ya"), "o4")
                     else:
-                        scores(0)
+                        upper_scores()
                 tt(plane("tw", b, a, e), plane("tw", b, a, e), bank(4 - 4 * h + b, H), A.add)
-                if h == 0 or b < 2:
+                if h == 1 or b < 2:
                     act(elems("xt", b, a, e), plane("tw", b, a, e), scale=1.0 / 32)
+                if h == 0 and not final:
+                    twin(b)
         for b in (2, 3):
-            ts(elems("xt", b, H, C), plane("tw", b, H, C), 1.0 / 32, A.mult)
-        if not final:
-            masked(0)
-        qstate(1)
+            ts(elems("xt", b, 0, H), plane("tw", b, 0, H), 1.0 / 32, A.mult)
+        qstate(0)
 
-    mm(bank(5, H), R("vq"), R("vs"), half("xq", 1), half("xs", 1))
-    store("y", T.oc[:, 2 * C:4 * C], raw(half("xq", 1)), half("xq", 1), "o6")
+    mm(bank(1, H), R("vq"), R("vs"), half("xq", 0), half("xs", 0))
+    store("y", T.oc[:, 0:2 * C], raw(half("xq", 0)), half("xq", 0), "o6")
     for k in range(4):
         store("s", T.osc[4 * k:4 * k + 4, :], T.xs[32 * k:32 * k + 4, :], R("xs"), "o3")
-    copy(R("yc"), bank(5, H))
-    store("y", T.y[:, H:C], ap(R("yc")), R("yc"), "o5")
+    copy(R("yc"), bank(1, H))
+    store("y", T.y[:, 0:H], ap(R("yc")), R("yc"), "o5")
     for sem in SEMAPHORES:
         if max(seen[q][sem] for q in queue) < count[sem]:
             wait("g", sem, count[sem])

@@ -4,28 +4,36 @@ from concourse.mybir import dt, AluOpType, AxisListType, ActivationFunctionType
 C, K, ROUNDS = 448, 128, 3
 F = C + K
 H = C // 2
+LAST = H
 NK = C // 16
 BIG = 2.0 ** 90
 OFF = 1024.0
 MID = 192.0
 NS = 7
+SUMS = (((), (4, 8, 5, 6, 7), (13, 11, 9, 12, 10)), ((7,), (4, 8, 5, 6), (13, 11, 9, 12, 10)))
 NP = (NK - 1 - NS) // 2
 WIDTH = [max(128, C - 64 * s) for s in range(7)]
 START = [sum(WIDTH[:s]) for s in range(8)]
 CODES, PLANE = "float8_e4m3fn_x4", "uint8"
 SMALL = ["wa", "td", "hh", "f2", "e1", "q", "e0", "qd", "cf", "ta", "tb", "th", "tz", "lo", "kl", "kk", "du", "tf"]
 
+FIRST = """sp pu yb pw a0 a1 ow osel ou border pm S2a S2b dd tz s1 b3 t1 send wa mo3 V2a V2b S3a S3b s0 td t0 f2 eq hh
+           V3a V3b th S4a S4b unpack """
+LATER = """sp pu yb pw a0 a1 ow pm S2a S2b osel s1 ou border t1 wa s0 mo3 V2a V2b S3a S3b dd tz send t0 f2 hh
+           V3a V3b th S4a S4b unpack td """
+REST = "s2 e1 e0 V4a q V4b qd s3 ta lo kl tb kk du tf tu"
+
 BUFFERS = {
-    "bfloat16": dict(xt=4 * C, ut=512, vt=512, ci=C, e0=K, e1=K, mask=C, dx=C, dsel=2 * C, dseg=C, dbc=2 * C, gq=512, gd=512,
-                     bd=512, one=2 * C, et0=516, et1=516, ew=516, uu=4 * START[7], sg=3 * C, rd=C, sp=2 * C, yb=2 * C,
-                     pw=2 * C + 16, bt=4 * K, pm=2 * C, c2=C, b2=C + 16, ca=C, z3=C, r0=C, rz=C, tw=4 * F, tc=4 * C,
-                     gw=4 * F, zt=4 * C),
-    "float32": dict(mf=2 * NK, mg=2 * NK, dm=2 * NK, pf=12, num=F, k16=NK, base=NK, mk=C, sc=C, acc=NS + NP, a1w=NK, a2w=NK,
-                    junk=192 * NP, p128=NK, dd=2 * NK, ow=C, osel=K, t0=2 * NK, t1=2 * NK, t3=2 * NK, otr=C, ya=H, yc=H,
+    "bfloat16": dict(xt=4 * C, ut=512, vt=512, ci=C, e0=K, e1=K, mask=C, dx=C, dsel=C, dbc=2 * C, alt=2 * C, gd=512,
+                     bd=512, one=516, et0=516, et1=516, ew=516, uu=4 * START[7], sg=3 * C, rd=C, sp=2 * C, yb=2 * C,
+                     pw=2 * C, bt=4 * K, pa=2 * C, pm=2 * C + 16, c2=C, b2=2 * C + 16, ca=C, z3=C, r0=C, rz=C, tw=4 * F,
+                     tc=4 * C, gw=4 * F, zt=4 * C),
+    "float32": dict(mf=2 * NK, mg=2 * NK, m2=2 * NK, dm=2 * NK, pf=12, k4=4, lim=4, num=F, k16=NK, base=NK, mk=C, sc=C, acc=NS + NP, a1w=NK, a2w=NK,
+                    junk=192 * NP, p128=NK, dd=NK, ow=C, osel=K, t0=2 * NK, t1=2 * NK, otr=C, ya=C - LAST, yc=LAST,
                     csel=C, sm=len(SMALL) * NK),
     "float16": dict(s1=2 * C, s2=C, s3=C),
     "int32": dict(uoi=8, mvt=2 * NK, mi=2 * NK, pi=4, rr=NK + NP),
-    "uint16": dict(uo=8, mo=2 * NK, mo2=2 * NK, mo3=NK, pu=NK, ou=8, tu=NK),
+    "uint16": dict(uo=8, mo=2 * NK, mo2=2 * NK, mo3=NK, mo4=NK, pu=NK, ou=8, tu=NK),
     CODES: dict(xq=C, uq0=128, uq=128, vq=128, wq=512, bq=384, eq=512, cq=START[7], zq=C, sq0=K, sq1=K, sq2=K, lq0=K, lq1=K, lq2=K),
     PLANE: dict(xs=C, us0=128, us=128, vs=128, wp=512, bs=384, es=512, cs=START[7], zs=C, ss0=K, ss1=K, ss2=K, ls0=K, ls1=K, ls2=K),
 }
@@ -33,7 +41,7 @@ SCRATCH = {name: ("sbuf", [128, n], kind) for kind in BUFFERS for name, n in BUF
 SCRATCH.update({"p%d" % b: ("psum", [128, 512], "float32") for b in range(8)})
 
 SEMAPHORES = ["cv", "ca", "ct", "cg", "lx", "lx2", "lu", "lm", "lw", "lp", "lv", "sent", "arr0", "arr1", "arr2",
-              "tw0", "tw1", "tw2", "tw3", "o1", "o2", "o3", "o4", "o5", "o6"]
+              "z0", "z1", "z2", "z3", "z4", "z5", "tw0", "tw1", "tw2", "tw3", "o1", "o2", "o3", "o4", "o5", "o6"]
 
 A = AluOpType
 ACT = ActivationFunctionType
@@ -191,58 +199,75 @@ def rank_program(g, core, T, topo):
     iota(col("pi", 0), [[0, 1]], 0, 1)
     iota(R("uoi"), [[16, 8]])
     iota(R("ci"), [[0, NK], [1, 16]])
-    iota(R("gq"), [[1, 8], [0, 64]])
-    fill(R("one"), 1.0)
-    where(R("et0"), R("one", 0, 516), [[1, 516]], A.is_equal, 0.0, -2, -4)
-    where(R("ew"), R("et0"), [[1, 516]], A.not_equal, 512.0, -3, -4)
+    iota(R("k4"), [[127, 2], [35, 2]], 1)
     iota(R("k16"), [[16, NK]])
+    fill(R("one"), 1.0)
+    where(R("et0"), R("one"), [[1, 516]], A.is_equal, 0.0, -2, -4)
+    where(R("ew"), R("et0"), [[1, 516]], A.not_equal, 512.0, -3, -4)
+    where(R("gd"), R("one", 0, 512), [[-16, 8], [0, 64]], A.is_ge, 0.0, 0, 1)
+    where(R("bd"), R("gd"), [[16, 8], [0, 64]], A.is_ge, 0.0, 15, -1)
+
+    def pad(s):
+        to = R("uu", 4 * (START[s] + C - 64 * s - 48), 4 * START[s + 1])
+        if s < 4:
+            act(to, R("one", 0, to[2] - to[1]), scale=0.0)
+        else:
+            iota(to, [[0, to[2] - to[1]]])
+
+    for s in (4, 5, 6):
+        pad(s)
+    where(half("dbc", 0, 2), R("one", 0, C), [[0, NK // 2], [1, 32]], A.is_gt, 0.0, 0, 0)
     iota(R("num"), [[1, F]])
-    where(R("dbc"), R("one"), [[0, NK], [1, 32]], A.is_gt, 0.0, 0, 0)
-    iota(R("sp"), [[0, 2 * C]])
-    where(R("et1"), R("one", 0, 516), [[1, 516]], A.is_equal, 0.0, -3, -4)
+    iota(half("alt", 0, 2), [[0, H], [4096, 2]], -4096)
+    where(R("et1"), R("one"), [[1, 516]], A.is_equal, 0.0, -3, -4)
 
     ts(col("pi", 1), col("pi", 0), 15, A.bitwise_and)
-    ts(col("pi", 2), col("pi", 0), 4, A.logical_shift_right)
     ts(col("pi", 3), col("pi", 0), 16, A.bitwise_and)
     copy(R("uo"), R("uoi"))
-    copy(R("pf", 0, 3), R("pi", 1, 4))
+    copy(R("pf", 0, 3, 2), R("pi", 1, 4, 2))
     fill(R("dx"), 0.0)
     ts(col("pf", 8), col("pf", 0), -BIG, A.mult)
     ts(col("pf", 9), col("pf", 0), 1.0, A.add)
     ts(col("pf", 3), col("pf", 0), 15.0, A.is_lt, OFF, A.mult)
     fill(R("dx", 0, C, 16), -32 * BIG)
-    for s in range(7):
-        fill(R("uu", 4 * (START[s] + C - 64 * s - 48), 4 * START[s + 1]), 0.0)
+    fill(col("rr", 0), 0)
+    for s in (2, 3, 0):
+        pad(s)
     act(R("mask"), R("ci"), ACT.Abs, col("pf", 8), BIG)
-    act(R("gd"), R("gq"), ACT.Abs, col("pf", 1), -1.0)
-    act(R("bd"), R("gd"), ACT.Relu, 1.0, -1.0)
+    pad(1)
+    ts(col("pf", 5), col("pf", 3), col("pf", 0), A.add)
+    ts(R("e0"), R("ci", 0, K), col("pf", 0), A.is_equal, -4 * OFF, A.mult)
+    ts(R("e1"), R("ci", 0, K), col("pf", 9), A.is_equal, OFF, A.mult)
+    ts(col("pf", 4), col("pf", 5), -1.0, A.mult, K + 15.0, A.add)
+    tt(R("dsel", 0, K), R("e0"), R("e1"), A.add)
+    ts(R("lim"), R("k4"), col("pf", 3), A.add)
+    fill(R("pm", 2 * C, 2 * C + 16), -200.0)
+    fill(R("b2", 2 * C, 2 * C + 16), -8.0)
+    ts(R("base"), R("k16"), col("pf", 4), A.add)
+    copy(R("mf"), R("mvt"))
+    ts(R("mi"), R("mvt"), 4, A.logical_shift_right)
     quant(R("uq0"), R("us0"), R("ut"))
+    copy(R("mo"), R("mvt"))
     op("v", lambda: V.tensor_copy(ap(R("uq")).bitcast(dt.uint32), ap(R("uq0")).bitcast(dt.uint32).indirect(ap(R("uo")))),
        [R("uq0"), R("uo")], [R("uq")])
     op("s", lambda: S.activation(ap(R("us")), ap((R("us0"), R("uo"))), ACT.Copy), [R("us0"), R("uo")], [R("us")])
-    ts(R("e0"), R("ci", 0, K), col("pf", 0), A.is_equal, -4 * OFF, A.mult)
-    ts(R("e1"), R("ci", 0, K), col("pf", 9), A.is_equal, OFF, A.mult)
-    act(R("dseg"), R("ci"), ACT.Sign)
-    for j, c in ((5, 128.0), (6, 1.0), (7, 35.5), (10, 4096.0)):
-        act(col("pf", j), col("pf", 3), ACT.Identity, c)
+    for b in range(3):
+        act(plane("tw", b, H, C), elems("xt", b, H, C), scale=32.0)
+    ts(R("mg"), R("mi"), 16.0, A.mult, col("pf", 2), A.add)
 
-    def later_constants(j):
-        if j == 0:
-            tt(R("dsel", 0, K), R("e0"), R("e1"), A.add)
-            ts(col("pf", 4), col("pf", 3), col("pf", 0), A.add, -(K + 15.0), A.add)
-            copy(R("dsel", K, 2 * K), R("dsel", 0, K))
-            fill(col("rr", 0), 0)
-            copy(R("dsel", 2 * K, C), R("dsel", 0, C - 2 * K))
-        else:
-            ts(R("base"), R("k16"), col("pf", 4), A.subtract)
-            fill(R("pw", 2 * C, 2 * C + 16), -200.0)
-            fill(R("b2", C, C + 16), -8.0)
-            copy(R("mo"), R("mvt"))
-            ts(R("mi"), R("mvt"), 4, A.logical_shift_right)
-            copy(R("mf"), R("mvt"))
-            ts(R("mg"), R("mi"), 16.0, A.mult, col("pf", 2), A.add)
-            tt(R("dm", 0, NK), R("mf", NK, 2 * NK), R("mf", 0, NK), A.subtract)
-            tt(R("t0"), R("mg"), R("mf"), A.add)
+    def move(to, src, sem):
+        op("y", lambda: g.sync.dma_start(ap(to), ap(src)), [src], [to], sem, 16)
+
+    move(R("dsel", K, 2 * K), R("dsel", 0, K), "z0")
+    move(R("dsel", 2 * K, C), R("dsel", 0, C - 2 * K), "z1")
+    for name, sem in (("sp", "z2"), ("b2", "z3")):
+        src = R("uu", 4 * START[7] - H, 4 * START[7])
+        for j in range(4):
+            move(half(name, j), src, sem)
+        mark(wrote, R(name, 0, 2 * C), sem, count[sem])
+    for name, sem in (("dbc", "z4"), ("alt", "z5")):
+        move(half(name, 1, 2), half(name, 0, 2), sem)
+
 
     def slot(sg, a, b):
         at = START[sg // 4]
@@ -285,8 +310,8 @@ def rank_program(g, core, T, topo):
             a = C - 16 * sg
             ts(slot(sg, 0, a), bank(1, a), col("sc", a + 15), A.is_lt)
 
-    def qstate(h):
-        quant(half("xq", h), half("xs", h), half("xt", h, 4))
+    def qstate(a, e):
+        quant(R("xq", a, e), R("xs", a, e), R("xt", 4 * a, 4 * e))
 
     def upper_scores():
         mm(bank(0, H), R("uq"), R("us"), half("xq", 1), half("xs", 1))
@@ -296,8 +321,7 @@ def rank_program(g, core, T, topo):
         return (win, R(lst, NK * k + a, NK * k + e))
 
     def twin(b):
-        to, src = R("tc", C * b, C * b + C), plane("tw", b)
-        op("y", lambda: g.sync.dma_start(ap(to), ap(src)), [src], [to], "tw%d" % b, 16)
+        move(R("tc", C * b, C * b + C), plane("tw", b), "tw%d" % b)
 
     def two(w):
         j = SMALL.index(w)
@@ -309,15 +333,16 @@ def rank_program(g, core, T, topo):
     for n in range(ROUNDS):
         first, final = n == 0, n == ROUNDS - 1
         if first:
-            qstate(1)
+            qstate(H, C)
             upper_scores()
-            later_constants(0)
-            qstate(0)
-        for b in (2, 1):
-            mm(bank(b, C), R("uq"), R("us"), R("xq"), R("xs"))
+            for k in range(2):
+                tt(R("dm", NK * k, NK * k + NK), m1, m0, A.subtract)
+            qstate(0, H)
+        for b, w in ((1, WIDTH[2]), (2, C)):
+            mm(bank(b, w), R("uq"), R("us"), R("xq", 0, w), R("xs", 0, w))
         tt(half("mk", 1), bank(0, H), half("mask", 1), A.subtract)
         if first:
-            quant(block("bq", 0), block("bs", 0), R("bd"))
+            ts(R("m2"), R("mf"), 2.0, A.mult, 1.0, A.add)
         scan(half("sc", 1), half("dx", 1), half("mk", 1))
         tt(half("mk", 0), bank(1, H), half("mask", 0), A.subtract)
         sign(1)
@@ -342,8 +367,11 @@ def rank_program(g, core, T, topo):
         mpair(7, 7, 2)
         sign(5)
         relu(4)
-        tt(slot(0, 0, C), bank(1, C), R("sc"), A.is_le)
+        for h in range(2):
+            tt(slot(0, H * h, H * h + H), bank(1 - h, H), half("sc", h), A.is_le)
         rows(16, 18)
+        if first:
+            quant(block("bq", 0), block("bs", 0), R("bd"))
         qtiles(0, C)
         for s in (0, 2, 3):
             mtile(s, start=s == 0)
@@ -358,103 +386,115 @@ def rank_program(g, core, T, topo):
         sign(7)
         relu(6)
         relu(7)
-        scan(R("rd"), R("dseg"), slot(0, 0, C), A.mult, A.add)
+        scan(R("rd"), R("ci"), slot(0, 0, C), A.min, A.add)
+        if n == 1:
+            quant(R("vq"), R("vs"), R("vt"))
         if first:
-            later_constants(1)
+            tt(R("t0"), R("mg"), R("mf"), A.add)
+            copy(R("mo4"), R("m2", 0, NK))
+            copy(R("mo2"), R("t0"))
+        tt(R("a1w"), R("base"), last("rd"), A.subtract)
+        early, by_s, late = SUMS[min(n, 1)]
+        for q in early:
+            spair(q, "v")
         qtiles(1, WIDTH[1])
         mtile(1, stop=True)
-        for q in (4, 5, 6, 7, 8):
+        for q in by_s:
             spair(q, "s")
-        for q in (13, 11, 9):
+        for q in late:
             spair(q, "v")
-        tt(R("a1w"), R("base"), last("rd"), A.subtract)
         scan(R("csel"), R("dsel", 0, C), bank(3, C))
-        for q in (12, 10):
-            spair(q, "v")
-        tt(R("a2w"), R("a1w"), last("csel"), A.add)
         copy(R("rr", NK - NS, NK + NP), R("acc"))
+        tt(R("a2w"), R("a1w"), last("csel"), A.add)
         ts(R("rr", 2, 2 * NP + 1, 2), R("rr", NK, NK + NP), 511, A.bitwise_and)
         ts(R("rr", 1, 2 * NP + 1, 2), R("rr", NK, NK + NP), 9, A.logical_shift_right)
         if first:
             for b in range(4):
-                act(plane("tw", b), elems("xt", b), scale=32.0)
+                e = H if b < 3 else C
+                act(plane("tw", b, 0, e), elems("xt", b, 0, e), scale=32.0)
                 twin(b)
-            act(R("dsel", C, 2 * C), R("dsel", 0, C))
-            act(R("dm", NK, 2 * NK), R("dm", 0, NK))
         tt(R("p128"), R("a2w"), R("rr", 0, NK), A.subtract)
         sq, ss, lq, ls, arr = R("sq%d" % n), R("ss%d" % n), R("lq%d" % n), R("ls%d" % n), "arr%d" % n
-        ts(R("pu"), R("p128"), -float(K), A.add)
-        for k in range(2):
-            act(R("dd", NK * k, NK * k + NK), R("p128"), ACT.Relu, -2048.0 * (C - 0.5), 2048.0)
-        act(W["tz"], R("dd", 0, NK), ACT.Identity, col("pf", 3))
-        ts(R("sp", 0, 2 * C, 32), R("p128"), -(K + MID), A.add, 128.0, A.min)
-        op("v", lambda: V.tensor_copy(ap((R("ow"), R("pu"))), ap(R("num", 0, C))), [R("num", 0, C), R("pu")], [R("ow")])
-        tt(W["td"], R("p128"), R("dd", 0, NK), A.min)
-        scan(R("osel"), R("dsel", 0, K), R("ow", 0, K))
-        tt(R("t3"), R("t0"), R("dd"), A.add)
-        ts(R("ou"), last("osel", 0, K), col("pf", 3), A.subtract)
-        for b in range(4):
-            act(elems("bt", b, 0, K), (plane("tw", b), R("ou")), scale=1.0 / 32)
-        scan(R("yb"), R("dbc"), R("sp"), A.mult, A.add)
-        ts(R("mo2"), R("t3"), 2.0 * C, A.min)
-        op("v", lambda: V.transpose(ap(R("pw", 0, 2 * C)), ap(R("yb"))), [R("yb")], [R("pw", 0, 2 * C)])
-        for h in range(2):
-            act(half("pm", h), moves(R("pw"), "mo2", 0, h))
-        quant(sq, ss, R("bt"))
-        before("g", [sq, ss], [])
-        rid, pid = topo.addr(dst)[0:2]
-        for to, src in ((lq, sq), (ls, ss)):
-            g.remote_dma(raw(to), raw(src), T.sem[arr], T.sem["sent"], pid, rid, topo.mask(core, dst))
-            count["sent"] += len(topo.engines(core, dst))
-            count[arr] += len(topo.engines(src_core, core))
-        mark(wrote, lq, arr, count[arr])
-        mark(wrote, ls, arr, count[arr])
-        won = R("pm", C, 2 * C)
-        for h in range(2):
-            tt(half("pm", 2 + h), moves(R("pw"), "mo2", 1, h), half("pm", h), A.max)
-        for h in range(2):
-            act(half("c2", h), moves(won, "mo", 0, h), ACT.Identity, 639.5, -4.0)
-        scan(R("s1"), R("dsel"), R("pm"))
-        ts(R("t1"), last("s1", 0, 2 * C), col("pf", 5), A.is_ge, 1024.0, A.mult)
-        tt(half("b2", 0), moves(won, "mo", 1, 0), half("c2", 0), A.is_ge)
-        tt(W["wa"], R("t1", NK, 2 * NK), m1, A.add)
-        tt(half("b2", 1), moves(won, "mo", 1, 1), half("c2", 1), A.is_ge)
-        for h in range(2):
-            act(half("ca", h), moves(R("b2"), "mo", 0, h), scale=2.0)
-        ts(R("mo3"), W["wa"], float(C), A.min)
-        tt(W["f2"], last("s1"), last("s1", C), A.is_equal)
-        tt(W["hh"], R("t1", NK, 2 * NK), R("t1", 0, NK), A.is_gt)
-        ts(W["th"], W["f2"], -4096.0, A.mult, col("pf", 10), A.add)
-        if first:
+
+        def border():
+            for b in range(4 - first):
+                act(elems("bt", b, 0, K), (plane("tw", b), R("ou")), scale=1.0 / 32)
+
+        def send():
+            quant(sq, ss, R("bt"))
+            before("g", [sq, ss], [])
+            rid, pid = topo.addr(dst)[0:2]
+            for to, src in ((lq, sq), (ls, ss)):
+                g.remote_dma(raw(to), raw(src), T.sem[arr], T.sem["sent"], pid, rid, topo.mask(core, dst))
+                count["sent"] += len(topo.engines(core, dst))
+                count[arr] += len(topo.engines(src_core, core))
+            mark(wrote, lq, arr, count[arr])
+            mark(wrote, ls, arr, count[arr])
+
+        def unpack():
             for b in range(4):
+                mm(bank(b, K), block("eq", b), block("es", b), lq, ls)
+            for name, scale in (("tw", 32.0), ("gw", 64.0)):
+                for b in range(4):
+                    act(plane(name, b, C, F), bank(b, K), scale=scale)
+
+        def unpackers():
+            for b in range(4 * first):
                 a = 2 - 2 * (b // 2)
                 quant(block("eq", b), block("es", b), R("et%d" % (b % 2), a, a + 512))
-        for h in range(2):
-            tt(half("z3", h), moves(R("b2"), "mo3", 0, h), half("ca", h), A.add)
-        for h in range(2):
-            act(half("r0", h), moves(R("z3"), "mo", 0, h), ACT.Square)
-        for b in range(4):
-            mm(bank(b, K), block("eq", b), block("es", b), lq, ls)
-        for b in range(4):
-            act(plane("tw", b, C, F), bank(b, K), scale=32.0)
-        for b in range(4):
-            act(plane("gw", b, C, F), bank(b, K), scale=64.0)
-        scan(R("s2"), R("dsel", 0, C), R("z3"))
-        ts(W["e1"], last("s2"), col("pf", 6), A.is_equal)
-        tt(W["e0"], last("s2"), W["tz"], A.is_equal)
-        tt(half("rz", 0), moves(R("z3"), "mo", 1, 0), half("r0", 0), A.mult)
-        tt(W["q"], W["e1"], W["hh"], A.add)
-        tt(half("rz", 1), moves(R("z3"), "mo", 1, 1), half("r0", 1), A.mult)
-        tt(two("qd"), two("q"), R("dm"), A.mult)
-        scan(R("s3"), R("dsel", 0, C), R("rz"))
-        tt(W["ta"], W["qd"], m0, A.add)
-        tt(W["lo"], last("s3"), W["th"], A.is_equal)
-        ts(W["kl"], last("s3"), col("pf", 7), A.is_ge)
-        tt(W["tb"], W["ta"], W["td"], A.max)
-        tt(W["kk"], W["lo"], W["kl"], A.add)
-        tt(W["du"], W["kk"], W["cf"], A.mult)
-        tt(W["tf"], W["du"], W["tb"], A.add)
-        copy(R("tu"), W["tf"])
+
+        def odd(name, h):
+            return R(name, C * h + 1, C * h + C, 2)
+
+        step = dict(
+            sp=lambda: ts(R("sp", 0, 2 * C, 32), R("p128"), -(K + MID), A.add, 128.0, A.min),
+            yb=lambda: scan(R("yb"), R("dbc"), R("sp"), A.mult, A.add),
+            pw=lambda: op("v", lambda: V.transpose(ap(R("pw")), ap(R("yb"))), [R("yb")], [R("pw")]),
+            pu=lambda: ts(R("pu"), R("p128"), -float(K), A.add),
+            ow=lambda: op("v", lambda: V.tensor_copy(ap((R("ow"), R("pu"))), ap(R("num", 0, C))), [R("num", 0, C), R("pu")], [R("ow")]),
+            osel=lambda: scan(R("osel"), R("dsel", 0, K), R("ow", 0, K)),
+            ou=lambda: ts(R("ou"), last("osel", 0, K), col("pf", 3), A.subtract),
+            b3=lambda: ts(elems("bt", 3, 0, K), (plane("tw", 3), R("ou")), 1.0 / 32, A.mult),
+            border=border, send=send, unpack=unpack, eq=unpackers,
+            dd=lambda: act(R("dd"), R("p128"), ACT.Relu, -2048.0 * (C - 0.5), 2048.0),
+            tz=lambda: act(W["tz"], R("dd"), ACT.Identity, col("pf", 3)),
+            td=lambda: tt(W["td"], R("p128"), R("dd"), A.min),
+            a0=lambda: act(R("pa", 0, 2 * C, 2), moves(R("pw"), "mo2", 0)),
+            a1=lambda: act(R("pa", 1, 2 * C, 2), moves(R("pw"), "mo2", 1)),
+            pm=lambda: scan(R("pm", 0, 2 * C), R("alt"), R("pa")),
+            s0=lambda: scan(R("s1", 0, C), R("dsel"), R("pa", 0, 2 * C, 2)),
+            s1=lambda: scan(R("s1", C, 2 * C), R("dsel"), R("pm", 1, 2 * C, 2)),
+            t0=lambda: ts(R("t1", 0, NK), last("s1"), col("lim", 2), A.is_ge, 1024.0, A.mult),
+            t1=lambda: ts(R("t1", NK, 2 * NK), last("s1", C), col("lim", 2), A.is_ge, 1024.0, A.mult),
+            wa=lambda: tt(W["wa"], R("t1", NK, 2 * NK), R("m2", NK, 2 * NK), A.add),
+            mo3=lambda: ts(R("mo3"), W["wa"], 2.0 * C, A.min),
+            f2=lambda: tt(W["f2"], last("s1"), last("s1", C), A.is_equal),
+            hh=lambda: tt(W["hh"], R("t1", NK, 2 * NK), R("t1", 0, NK), A.is_gt),
+            th=lambda: act(W["th"], W["f2"], ACT.Identity, col("lim", 3), -163.0),
+            s2=lambda: scan(R("s2"), R("dsel"), R("z3")),
+            e1=lambda: ts(W["e1"], last("s2"), col("lim", 0), A.is_equal),
+            e0=lambda: tt(W["e0"], last("s2"), W["tz"], A.is_equal),
+            q=lambda: tt(W["q"], W["e1"], W["hh"], A.add),
+            qd=lambda: tt(two("qd"), two("q"), R("dm"), A.mult),
+            ta=lambda: tt(W["ta"], W["qd"], m0, A.add),
+            tb=lambda: tt(W["tb"], W["ta"], W["td"], A.max),
+            s3=lambda: scan(R("s3"), R("dsel"), R("rz")),
+            lo=lambda: tt(W["lo"], last("s3"), W["th"], A.is_equal),
+            kl=lambda: ts(W["kl"], last("s3"), col("lim", 1), A.is_ge),
+            kk=lambda: tt(W["kk"], W["lo"], W["kl"], A.add),
+            du=lambda: tt(W["du"], W["kk"], W["cf"], A.mult),
+            tf=lambda: tt(W["tf"], W["du"], W["tb"], A.add),
+            tu=lambda: copy(R("tu"), W["tf"]))
+        for h, x in enumerate("ab"):
+            step.update({
+                "S2" + x: lambda h=h: act(half("c2", h), moves(R("pm"), "mo4", 0, h), ACT.Identity, 639.5, -4.0),
+                "V2" + x: lambda h=h: tt(odd("b2", h), moves(R("pm"), "mo3", 0, h), half("c2", h), A.is_ge),
+                "S3" + x: lambda h=h: act(half("ca", h), moves(R("b2"), "mo4", 0, h), scale=2.0),
+                "V3" + x: lambda h=h: tt(half("z3", h), moves(R("b2"), "mo3", 0, h), half("ca", h), A.add),
+                "S4" + x: lambda h=h: act(half("r0", h), moves(R("z3"), "mo", 0, h), ACT.Square),
+                "V4" + x: lambda h=h: tt(half("rz", h), moves(R("z3"), "mo", 1, h), half("r0", h), A.mult)})
+        for w in ((FIRST if first else LATER) + REST).split():
+            step[w]()
         for b in range(4):
             tt(plane("gw", b), moves(plane("tw", b, 0, F), "tu", 0), R("tc", C * b, C * b + C), A.add)
             if b < 3:
@@ -464,39 +504,36 @@ def rank_program(g, core, T, topo):
         if final:
             act(R("otr"), moves(R("num"), "tu", 0))
             store("y", T.ot[:], T.otr[0:128:16, :], R("otr"), "o1")
-        for h in (1, 0):
-            quant(half("zq", h), half("zs", h), half("zt", h, 4))
+        cut = LAST if final else H
+        for h, a, e in ((1, cut, C), (0, 0, cut)):
+            quant(R("zq", a, e), R("zs", a, e), R("zt", 4 * a, 4 * e))
             for b in range(4):
-                mm(bank(4 - 4 * h + b, H), block("wq", b), block("wp", b), half("zq", h), half("zs", h))
-        if first:
-            quant(R("vq"), R("vs"), R("vt"))
-        for h in (1, 0):
-            a, e = H * h, H * h + H
+                mm(bank(4 - 4 * h + b, e - a), block("wq", b), block("wp", b), R("zq", a, e), R("zs", a, e))
+        for h, a, e in ((1, cut, C), (0, 0, cut)):
             for b in range(4):
-                if h == 0 and b == 3:
-                    qstate(1)
-                    if final:
-                        mm(bank(0, H), R("vq"), R("vs"), half("xq", 1), half("xs", 1))
-                        store("y", T.oc[:, 2 * C:4 * C], raw(half("xq", 1)), half("xq", 1), "o2")
-                        act(R("ya"), bank(0, H))
-                        store("s", T.y[:, H:C], ap(R("ya")), R("ya"), "o4")
-                    else:
-                        upper_scores()
-                tt(plane("tw", b, a, e), plane("tw", b, a, e), bank(4 - 4 * h + b, H), A.add)
+                tt(plane("tw", b, a, e), plane("tw", b, a, e), bank(4 - 4 * h + b, e - a), A.add)
                 if h == 1 or b < 2:
                     act(elems("xt", b, a, e), plane("tw", b, a, e), scale=1.0 / 32)
                 if h == 0 and not final:
                     twin(b)
+        qstate(cut, C)
+        if final:
+            mm(bank(0, C - cut), R("vq"), R("vs"), R("xq", cut), R("xs", cut))
+            store("y", T.oc[:, 4 * cut:4 * C], raw(R("xq", cut)), R("xq", cut), "o2")
+            act(R("ya"), bank(0, C - cut))
+            store("s", T.y[:, cut:C], ap(R("ya")), R("ya"), "o4")
+        else:
+            upper_scores()
         for b in (2, 3):
-            ts(elems("xt", b, 0, H), plane("tw", b, 0, H), 1.0 / 32, A.mult)
-        qstate(0)
+            ts(elems("xt", b, 0, cut), plane("tw", b, 0, cut), 1.0 / 32, A.mult)
+        qstate(0, cut)
 
-    mm(bank(1, H), R("vq"), R("vs"), half("xq", 0), half("xs", 0))
-    store("y", T.oc[:, 0:2 * C], raw(half("xq", 0)), half("xq", 0), "o6")
+    mm(bank(1, LAST), R("vq"), R("vs"), R("xq", 0, LAST), R("xs", 0, LAST))
+    store("s", T.oc[:, 0:4 * LAST], raw(R("xq", 0, LAST)), R("xq", 0, LAST), "o6")
     for k in range(4):
-        store("s", T.osc[4 * k:4 * k + 4, :], T.xs[32 * k:32 * k + 4, :], R("xs"), "o3")
-    copy(R("yc"), bank(1, H))
-    store("y", T.y[:, 0:H], ap(R("yc")), R("yc"), "o5")
+        store("sy"[k % 2], T.osc[4 * k:4 * k + 4, :], T.xs[32 * k:32 * k + 4, :], R("xs"), "o3")
+    copy(R("yc"), bank(1, LAST))
+    store("y", T.y[:, 0:LAST], ap(R("yc")), R("yc"), "o5")
     for sem in SEMAPHORES:
         if max(seen[q][sem] for q in queue) < count[sem]:
             wait("g", sem, count[sem])

@@ -10,28 +10,28 @@ BIG = 2.0 ** 90
 OFF = 1024.0
 MID = 192.0
 NS = 7
-SUMS = (((), (4, 8, 5, 6, 7), (13, 11, 9, 12, 10)), ((7,), (4, 8, 5, 6), (13, 11, 9, 12, 10)))
+SUMS = (((7,), (4, 8, 5, 6), (13, 11, 9, 12, 10)), ((6, 7), (4, 8, 5), (13, 11, 9, 12, 10)))
 NP = (NK - 1 - NS) // 2
 WIDTH = [max(128, C - 64 * s) for s in range(7)]
 START = [sum(WIDTH[:s]) for s in range(8)]
 CODES, PLANE = "float8_e4m3fn_x4", "uint8"
-SMALL = ["wa", "td", "hh", "f2", "e1", "q", "e0", "qd", "cf", "ta", "tb", "th", "tz", "lo", "kl", "kk", "du", "tf"]
+STEPS = 7
 
-FIRST = """sp pu yb pw a0 a1 ow osel ou border pm S2a S2b dd tz s1 b3 t1 send wa mo3 V2a V2b S3a S3b s0 td t0 f2 eq hh
-           V3a V3b th S4a S4b unpack """
-LATER = """sp pu yb pw a0 a1 ow pm S2a S2b osel s1 ou border t1 wa s0 mo3 V2a V2b S3a S3b dd tz send t0 f2 hh
-           V3a V3b th S4a S4b unpack td """
-REST = "s2 e1 e0 V4a q V4b qd s3 ta lo kl tb kk du tf tu"
+FIRST = """sp pu yba ybb pwa pwb a0 a1 ow s0 osel pma ou pmb border S2a S2b pt dd s1a s1b t1 b3 wa f2 mo3 send V2a V2b
+           S3a S3b nl np eq """
+LATER = """sp pu pt dd nl np yba ybb pwa pwb a0 a1 ow s0 osel pma ou pmb border S2a S2b s1a s1b t1 b3 wa f2 mo3 send V2a V2b
+           S3a S3b vq """
+REST = "hh V3a V3b S4a S4b unpack s2a s2b V4a e1 V4b s3a e0 s3b loa kla lob klb tfa tfb tua tub g0a g0b"
 
 BUFFERS = {
-    "bfloat16": dict(xt=4 * C, ut=512, vt=512, ci=C, e0=K, e1=K, mask=C, dx=C, dsel=C, dbc=2 * C, alt=2 * C, gd=512,
-                     bd=512, one=516, et0=516, et1=516, ew=516, uu=4 * START[7], sg=3 * C, rd=C, sp=2 * C, yb=2 * C,
+    "bfloat16": dict(xt=4 * C, ut=512, vt=512, ci=H, e0=K, e1=K, mask=H, dx=H, dsel=C, dbc=C, alt=C, gd=512,
+                     bd=512, nil=516, et0=516, et1=516, ew=516, uu=4 * START[7], sg=3 * C, cj=C, sp=2 * C, yb=2 * C,
                      pw=2 * C, bt=4 * K, pa=2 * C, pm=2 * C + 16, c2=C, b2=2 * C + 16, ca=C, z3=C, r0=C, rz=C, tw=4 * F,
                      tc=4 * C, gw=4 * F, zt=4 * C),
-    "float32": dict(mf=2 * NK, mg=2 * NK, m2=2 * NK, dm=2 * NK, pf=12, k4=4, lim=4, num=F, k16=NK, base=NK, mk=C, sc=C, acc=NS + NP, a1w=NK, a2w=NK,
-                    junk=192 * NP, p128=NK, dd=NK, ow=C, osel=K, t0=2 * NK, t1=2 * NK, otr=C, ya=C - LAST, yc=LAST,
-                    csel=C, sm=len(SMALL) * NK),
-    "float16": dict(s1=2 * C, s2=C, s3=C),
+    "float32": dict(w0=2 * NK, w1=2 * NK, wa=2 * NK, pf=12, k4=4, lim=4, kc=4, off=4, num=F, mk=C, sc=C, acc=NS + NP, a2w=NK, pl=NK,
+                    junk=192 * NP, dd=NK, ow=C, osel=K, t0=2 * NK, otr=C, ya=C - LAST, yc=LAST,
+                    csel=C, times=STEPS * NK, plus=STEPS * NK, tf=STEPS * NK),
+    "float16": dict(rd=C, s1=2 * C, s2=C, s3=C),
     "int32": dict(uoi=8, mvt=2 * NK, mi=2 * NK, pi=4, rr=NK + NP),
     "uint16": dict(uo=8, mo=2 * NK, mo2=2 * NK, mo3=NK, mo4=NK, pu=NK, ou=8, tu=NK),
     CODES: dict(xq=C, uq0=128, uq=128, vq=128, wq=512, bq=384, eq=512, cq=START[7], zq=C, sq0=K, sq1=K, sq2=K, lq0=K, lq1=K, lq2=K),
@@ -41,7 +41,7 @@ SCRATCH = {name: ("sbuf", [128, n], kind) for kind in BUFFERS for name, n in BUF
 SCRATCH.update({"p%d" % b: ("psum", [128, 512], "float32") for b in range(8)})
 
 SEMAPHORES = ["cv", "ca", "ct", "cg", "lx", "lx2", "lu", "lm", "lw", "lp", "lv", "sent", "arr0", "arr1", "arr2",
-              "z0", "z1", "z2", "z3", "z4", "z5", "tw0", "tw1", "tw2", "tw3", "o1", "o2", "o3", "o4", "o5", "o6"]
+              "z0", "z1", "z2", "z3", "y4", "y5", "y6", "tw0", "tw1", "tw2", "tw3", "o1", "o2", "o3", "o4", "o5", "o6"]
 
 A = AluOpType
 ACT = ActivationFunctionType
@@ -136,6 +136,9 @@ def rank_program(g, core, T, topo):
     def total(out, in_):
         op("v", lambda: V.tensor_reduce(ap(out), ap(in_), AxisListType.X, A.add), [in_], [out])
 
+    def turn(out, in_):
+        op("v", lambda: V.transpose(ap(out), ap(in_)), [in_], [out])
+
     def fill(out, val):
         op("v", lambda: V.memset(ap(out), val), [], [out])
 
@@ -187,86 +190,87 @@ def rank_program(g, core, T, topo):
     def bank(b, n, a=0):
         return R("p%d" % b, a, n)
 
+    def times(j):
+        return R("times", j, STEPS * NK, STEPS)
+
+    def plus(j):
+        return R("plus", j, STEPS * NK, STEPS)
+
     load("s", R("ut"), T.u[:], "lu")
     load("y", half("xt", 1, 4), T.x[:, 2 * C:4 * C], "lx")
     load("y", half("xt", 0, 4), T.x[:, 0:2 * C], "lx2")
     load("s", R("mvt"), T.mv[:], "lm")
     before("y", [R("xt")], [])
-    load("y", R("wq"), T.wc[:], "lw")
-    load("y", R("wp"), T.ws[:], "lp")
-    load("y", R("vt"), T.v[:], "lv")
 
     iota(col("pi", 0), [[0, 1]], 0, 1)
     iota(R("uoi"), [[16, 8]])
-    iota(R("ci"), [[0, NK], [1, 16]])
+    iota(R("ci", 0, K + 16), [[0, K // 16 + 1], [1, 16]])
+    iota(R("ci", K + 16, H), [[0, (H - K) // 16 - 1], [1, 16]])
     iota(R("k4"), [[127, 2], [35, 2]], 1)
-    iota(R("k16"), [[16, NK]])
-    fill(R("one"), 1.0)
-    where(R("et0"), R("one"), [[1, 516]], A.is_equal, 0.0, -2, -4)
+    iota(R("kc"), [[320, 2], [192, 2]], 15 - int(MID))
+    fill(R("nil"), 0.0)
+    where(R("dx"), R("nil", 0, H), [[0, NK // 2], [1, 16]], A.not_equal, -32 * BIG, 0, 0)
+    where(R("et0"), R("nil"), [[1, 516]], A.not_equal, 1.0, -2, -4)
     where(R("ew"), R("et0"), [[1, 516]], A.not_equal, 512.0, -3, -4)
-    where(R("gd"), R("one", 0, 512), [[-16, 8], [0, 64]], A.is_ge, 0.0, 0, 1)
+    where(R("gd"), R("nil", 0, 512), [[16, 8], [0, 64]], A.is_gt, 1.0, 0, -1)
     where(R("bd"), R("gd"), [[16, 8], [0, 64]], A.is_ge, 0.0, 15, -1)
+    iota(R("cj"), [[-16, NK], [1024, 16]])
+    iota(col("rr", 0), [[0, 1]])
+    where(half("dbc", 0, 2), R("nil", 0, C), [[0, NK // 2], [1, 32]], A.is_equal, 1.0, 0, 0)
+    where(R("times"), R("nil", 0, STEPS * NK), [[0, NK], [1, STEPS]], A.is_equal, 1.0, 0, 0)
+    iota(R("num"), [[1, F]])
+    iota(half("alt", 0, 2), [[0, H], [4096, 2]], -4096)
+    iota(R("w0"), [[0, NK], [1024, 2]])
+    iota(R("pm", 2 * C, 2 * C + 16), [[0, 16]], -200)
+    iota(R("b2", 2 * C, 2 * C + 16), [[0, 16]], -8)
+    where(R("et1"), R("nil"), [[1, 516]], A.not_equal, 1.0, -3, -4)
+
+    def move(to, src, sem):
+        op("y", lambda: g.sync.dma_start(ap(to), ap(src)), [src], [to], sem, 16)
 
     def pad(s):
         to = R("uu", 4 * (START[s] + C - 64 * s - 48), 4 * START[s + 1])
         if s < 4:
-            act(to, R("one", 0, to[2] - to[1]), scale=0.0)
+            act(to, R("nil", 0, to[2] - to[1]))
         else:
-            iota(to, [[0, to[2] - to[1]]])
-
-    for s in (4, 5, 6):
-        pad(s)
-    where(half("dbc", 0, 2), R("one", 0, C), [[0, NK // 2], [1, 32]], A.is_gt, 0.0, 0, 0)
-    iota(R("num"), [[1, F]])
-    iota(half("alt", 0, 2), [[0, H], [4096, 2]], -4096)
-    where(R("et1"), R("one"), [[1, 516]], A.is_equal, 0.0, -3, -4)
+            move(to, R("nil", 0, to[2] - to[1]), "y%d" % s)
 
     ts(col("pi", 1), col("pi", 0), 15, A.bitwise_and)
     ts(col("pi", 3), col("pi", 0), 16, A.bitwise_and)
     copy(R("uo"), R("uoi"))
     copy(R("pf", 0, 3, 2), R("pi", 1, 4, 2))
-    fill(R("dx"), 0.0)
-    ts(col("pf", 8), col("pf", 0), -BIG, A.mult)
-    ts(col("pf", 9), col("pf", 0), 1.0, A.add)
-    ts(col("pf", 3), col("pf", 0), 15.0, A.is_lt, OFF, A.mult)
-    fill(R("dx", 0, C, 16), -32 * BIG)
-    fill(col("rr", 0), 0)
+    ts(col("pf", 8), col("pi", 1), -BIG, A.mult)
+    ts(col("pf", 3), col("pi", 1), 15.0, A.is_lt, OFF, A.mult)
     for s in (2, 3, 0):
         pad(s)
     act(R("mask"), R("ci"), ACT.Abs, col("pf", 8), BIG)
     pad(1)
-    ts(col("pf", 5), col("pf", 3), col("pf", 0), A.add)
     ts(R("e0"), R("ci", 0, K), col("pf", 0), A.is_equal, -4 * OFF, A.mult)
-    ts(R("e1"), R("ci", 0, K), col("pf", 9), A.is_equal, OFF, A.mult)
-    ts(col("pf", 4), col("pf", 5), -1.0, A.mult, K + 15.0, A.add)
+    ts(R("e1"), R("ci", 15, K + 15), col("pf", 0), A.is_equal, OFF, A.mult)
     tt(R("dsel", 0, K), R("e0"), R("e1"), A.add)
-    ts(R("lim"), R("k4"), col("pf", 3), A.add)
-    fill(R("pm", 2 * C, 2 * C + 16), -200.0)
-    fill(R("b2", 2 * C, 2 * C + 16), -8.0)
-    ts(R("base"), R("k16"), col("pf", 4), A.add)
-    copy(R("mf"), R("mvt"))
-    ts(R("mi"), R("mvt"), 4, A.logical_shift_right)
-    quant(R("uq0"), R("us0"), R("ut"))
+    ts(R("mi"), R("mvt"), 512 - 16, A.bitwise_and)
     copy(R("mo"), R("mvt"))
+    ts(R("lim"), R("k4"), col("pf", 3), A.add)
+    tt(R("t0"), R("mi"), R("mvt"), A.add)
+    quant(R("uq0"), R("us0"), R("ut"))
+    ts(R("off"), R("kc"), col("pf", 3), A.subtract, col("pf", 0), A.subtract)
     op("v", lambda: V.tensor_copy(ap(R("uq")).bitcast(dt.uint32), ap(R("uq0")).bitcast(dt.uint32).indirect(ap(R("uo")))),
        [R("uq0"), R("uo")], [R("uq")])
     op("s", lambda: S.activation(ap(R("us")), ap((R("us0"), R("uo"))), ACT.Copy), [R("us0"), R("uo")], [R("us")])
-    for b in range(3):
+    for b in range(2):
         act(plane("tw", b, H, C), elems("xt", b, H, C), scale=32.0)
-    ts(R("mg"), R("mi"), 16.0, A.mult, col("pf", 2), A.add)
 
-    def move(to, src, sem):
-        op("y", lambda: g.sync.dma_start(ap(to), ap(src)), [src], [to], sem, 16)
-
+    for s in (4, 5, 6):
+        pad(s)
+    load("y", R("wq"), T.wc[:], "lw")
+    load("y", R("wp"), T.ws[:], "lp")
+    load("y", R("vt"), T.v[:], "lv")
     move(R("dsel", K, 2 * K), R("dsel", 0, K), "z0")
     move(R("dsel", 2 * K, C), R("dsel", 0, C - 2 * K), "z1")
     for name, sem in (("sp", "z2"), ("b2", "z3")):
-        src = R("uu", 4 * START[7] - H, 4 * START[7])
-        for j in range(4):
-            move(half(name, j), src, sem)
+        for j in range(2):
+            move(half(name, j, 2), R("nil", 0, C), sem)
         mark(wrote, R(name, 0, 2 * C), sem, count[sem])
-    for name, sem in (("dbc", "z4"), ("alt", "z5")):
-        move(half(name, 1, 2), half(name, 0, 2), sem)
 
 
     def slot(sg, a, b):
@@ -323,28 +327,22 @@ def rank_program(g, core, T, topo):
     def twin(b):
         move(R("tc", C * b, C * b + C), plane("tw", b), "tw%d" % b)
 
-    def two(w):
-        j = SMALL.index(w)
-        return R("sm", NK * j, NK * j + 2 * NK)
-
-    W = {w: R("sm", NK * j, NK * j + NK) for j, w in enumerate(SMALL)}
-    m0, m1 = R("mf", 0, NK), R("mf", NK, 2 * NK)
+    m0, m1, p128 = R("mvt", 0, NK), R("mvt", NK, 2 * NK), plus(6)
 
     for n in range(ROUNDS):
         first, final = n == 0, n == ROUNDS - 1
         if first:
             qstate(H, C)
             upper_scores()
-            for k in range(2):
-                tt(R("dm", NK * k, NK * k + NK), m1, m0, A.subtract)
+            ts(R("mo2"), R("t0"), col("pf", 2), A.add)
             qstate(0, H)
         for b, w in ((1, WIDTH[2]), (2, C)):
             mm(bank(b, w), R("uq"), R("us"), R("xq", 0, w), R("xs", 0, w))
-        tt(half("mk", 1), bank(0, H), half("mask", 1), A.subtract)
+        tt(half("mk", 1), bank(0, H), R("mask"), A.subtract)
         if first:
-            ts(R("m2"), R("mf"), 2.0, A.mult, 1.0, A.add)
-        scan(half("sc", 1), half("dx", 1), half("mk", 1))
-        tt(half("mk", 0), bank(1, H), half("mask", 0), A.subtract)
+            ts(R("w1", 1, 2 * NK, 2), m1, 2.0, A.mult, 1.0, A.add)
+        scan(half("sc", 1), R("dx"), half("mk", 1))
+        tt(half("mk", 0), bank(1, H), R("mask"), A.subtract)
         sign(1)
         sign(2)
         relu(1)
@@ -353,15 +351,15 @@ def rank_program(g, core, T, topo):
         sign(4)
         relu(3)
         rows(8, 10)
-        scan(half("sc", 0), half("dx", 0), half("mk", 0))
-        rows(10, 12)
+        scan(half("sc", 0), R("dx"), half("mk", 0))
+        rows(10, 13)
         if first:
             for j in range(2):
                 quant(block("bq", 1 + j), block("bs", 1 + j), R("ew", 2 - 2 * j, 514 - 2 * j))
         qtiles(2, WIDTH[2])
         mpair(4, 4, 2)
         mpair(5, 5, 2)
-        rows(12, 16)
+        rows(13, 17)
         qtiles(3, WIDTH[3])
         mpair(6, 6, 2)
         mpair(7, 7, 2)
@@ -369,13 +367,14 @@ def rank_program(g, core, T, topo):
         relu(4)
         for h in range(2):
             tt(slot(0, H * h, H * h + H), bank(1 - h, H), half("sc", h), A.is_le)
-        rows(16, 18)
+        rows(17, 18)
         if first:
             quant(block("bq", 0), block("bs", 0), R("bd"))
         qtiles(0, C)
         for s in (0, 2, 3):
             mtile(s, start=s == 0)
         rows(18, 28)
+        scan(R("rd"), R("cj"), slot(0, 0, C), A.min, A.add)
         qtiles(4, 448 if first else 384)
         for j in range(2):
             mcount(j, 1 + j, START[4], 384)
@@ -386,14 +385,8 @@ def rank_program(g, core, T, topo):
         sign(7)
         relu(6)
         relu(7)
-        scan(R("rd"), R("ci"), slot(0, 0, C), A.min, A.add)
-        if n == 1:
-            quant(R("vq"), R("vs"), R("vt"))
         if first:
-            tt(R("t0"), R("mg"), R("mf"), A.add)
-            copy(R("mo4"), R("m2", 0, NK))
-            copy(R("mo2"), R("t0"))
-        tt(R("a1w"), R("base"), last("rd"), A.subtract)
+            ts(R("mo4"), m0, 2.0, A.mult, 1.0, A.add)
         early, by_s, late = SUMS[min(n, 1)]
         for q in early:
             spair(q, "v")
@@ -403,21 +396,21 @@ def rank_program(g, core, T, topo):
             spair(q, "s")
         for q in late:
             spair(q, "v")
-        scan(R("csel"), R("dsel", 0, C), bank(3, C))
         copy(R("rr", NK - NS, NK + NP), R("acc"))
-        tt(R("a2w"), R("a1w"), last("csel"), A.add)
+        scan(R("csel"), R("dsel", 0, C), bank(3, C))
         ts(R("rr", 2, 2 * NP + 1, 2), R("rr", NK, NK + NP), 511, A.bitwise_and)
         ts(R("rr", 1, 2 * NP + 1, 2), R("rr", NK, NK + NP), 9, A.logical_shift_right)
+        tt(R("a2w"), last("csel"), last("rd"), A.subtract)
         if first:
             for b in range(4):
-                e = H if b < 3 else C
+                e = H if b < 2 else C
                 act(plane("tw", b, 0, e), elems("xt", b, 0, e), scale=32.0)
                 twin(b)
-        tt(R("p128"), R("a2w"), R("rr", 0, NK), A.subtract)
+        tt(R("pl"), R("a2w"), R("rr", 0, NK), A.subtract)
         sq, ss, lq, ls, arr = R("sq%d" % n), R("ss%d" % n), R("lq%d" % n), R("ls%d" % n), "arr%d" % n
 
         def border():
-            for b in range(4 - first):
+            for b in range(3):
                 act(elems("bt", b, 0, K), (plane("tw", b), R("ou")), scale=1.0 / 32)
 
         def send():
@@ -442,51 +435,50 @@ def rank_program(g, core, T, topo):
             for b in range(4 * first):
                 a = 2 - 2 * (b // 2)
                 quant(block("eq", b), block("es", b), R("et%d" % (b % 2), a, a + 512))
+            if first:
+                tt(times(4), m1, m0, A.subtract)
+                copy(plus(4), m0)
 
         def odd(name, h):
             return R(name, C * h + 1, C * h + C, 2)
 
         step = dict(
-            sp=lambda: ts(R("sp", 0, 2 * C, 32), R("p128"), -(K + MID), A.add, 128.0, A.min),
-            yb=lambda: scan(R("yb"), R("dbc"), R("sp"), A.mult, A.add),
-            pw=lambda: op("v", lambda: V.transpose(ap(R("pw")), ap(R("yb"))), [R("yb")], [R("pw")]),
-            pu=lambda: ts(R("pu"), R("p128"), -float(K), A.add),
+            sp=lambda: ts(R("sp", 0, 2 * C, 32), R("pl"), col("off", 0), A.add, 128.0, A.min),
+            pu=lambda: ts(R("pu"), R("pl"), col("off", 1), A.add),
+            pt=lambda: act(p128, R("pl"), ACT.Identity, col("off", 2)),
             ow=lambda: op("v", lambda: V.tensor_copy(ap((R("ow"), R("pu"))), ap(R("num", 0, C))), [R("num", 0, C), R("pu")], [R("ow")]),
             osel=lambda: scan(R("osel"), R("dsel", 0, K), R("ow", 0, K)),
             ou=lambda: ts(R("ou"), last("osel", 0, K), col("pf", 3), A.subtract),
             b3=lambda: ts(elems("bt", 3, 0, K), (plane("tw", 3), R("ou")), 1.0 / 32, A.mult),
             border=border, send=send, unpack=unpack, eq=unpackers,
-            dd=lambda: act(R("dd"), R("p128"), ACT.Relu, -2048.0 * (C - 0.5), 2048.0),
-            tz=lambda: act(W["tz"], R("dd"), ACT.Identity, col("pf", 3)),
-            td=lambda: tt(W["td"], R("p128"), R("dd"), A.min),
+            vq=lambda: quant(R("vq"), R("vs"), R("vt")) if n == 1 else None,
+            dd=lambda: act(R("dd"), p128, ACT.Relu, -2048.0 * (C - 0.5), 2048.0),
+            nl=lambda: act(times(6), R("dd"), ACT.Relu, 1.0, -1.0),
+            np=lambda: act(plus(5), p128, scale=-1.0),
             a0=lambda: act(R("pa", 0, 2 * C, 2), moves(R("pw"), "mo2", 0)),
             a1=lambda: act(R("pa", 1, 2 * C, 2), moves(R("pw"), "mo2", 1)),
-            pm=lambda: scan(R("pm", 0, 2 * C), R("alt"), R("pa")),
             s0=lambda: scan(R("s1", 0, C), R("dsel"), R("pa", 0, 2 * C, 2)),
-            s1=lambda: scan(R("s1", C, 2 * C), R("dsel"), R("pm", 1, 2 * C, 2)),
-            t0=lambda: ts(R("t1", 0, NK), last("s1"), col("lim", 2), A.is_ge, 1024.0, A.mult),
-            t1=lambda: ts(R("t1", NK, 2 * NK), last("s1", C), col("lim", 2), A.is_ge, 1024.0, A.mult),
-            wa=lambda: tt(W["wa"], R("t1", NK, 2 * NK), R("m2", NK, 2 * NK), A.add),
-            mo3=lambda: ts(R("mo3"), W["wa"], 2.0 * C, A.min),
-            f2=lambda: tt(W["f2"], last("s1"), last("s1", C), A.is_equal),
-            hh=lambda: tt(W["hh"], R("t1", NK, 2 * NK), R("t1", 0, NK), A.is_gt),
-            th=lambda: act(W["th"], W["f2"], ACT.Identity, col("lim", 3), -163.0),
-            s2=lambda: scan(R("s2"), R("dsel"), R("z3")),
-            e1=lambda: ts(W["e1"], last("s2"), col("lim", 0), A.is_equal),
-            e0=lambda: tt(W["e0"], last("s2"), W["tz"], A.is_equal),
-            q=lambda: tt(W["q"], W["e1"], W["hh"], A.add),
-            qd=lambda: tt(two("qd"), two("q"), R("dm"), A.mult),
-            ta=lambda: tt(W["ta"], W["qd"], m0, A.add),
-            tb=lambda: tt(W["tb"], W["ta"], W["td"], A.max),
-            s3=lambda: scan(R("s3"), R("dsel"), R("rz")),
-            lo=lambda: tt(W["lo"], last("s3"), W["th"], A.is_equal),
-            kl=lambda: ts(W["kl"], last("s3"), col("lim", 1), A.is_ge),
-            kk=lambda: tt(W["kk"], W["lo"], W["kl"], A.add),
-            du=lambda: tt(W["du"], W["kk"], W["cf"], A.mult),
-            tf=lambda: tt(W["tf"], W["du"], W["tb"], A.add),
-            tu=lambda: copy(R("tu"), W["tf"]))
+            t1=lambda: ts(R("w1", 0, 2 * NK, 2), last("s1", C), col("lim", 2), A.is_ge),
+            wa=lambda: scan(R("wa"), R("w0"), R("w1"), A.mult, A.add),
+            mo3=lambda: ts(R("mo3"), R("wa", 1, 2 * NK, 2), 2.0 * C, A.min),
+            f2=lambda: tt(times(1), last("s1"), last("s1", C), A.is_equal),
+            hh=lambda: tt(plus(2), R("w1", 0, 2 * NK, 2), times(1), A.is_gt),
+            e1=lambda: ts(plus(3), last("s2"), col("lim", 0), A.is_equal),
+            e0=lambda: ts(times(2), last("s2"), col("pf", 3), A.is_equal))
         for h, x in enumerate("ab"):
+            a, e = STEPS * NK // 2 * h, STEPS * NK // 2 * (h + 1)
             step.update({
+                "yb" + x: lambda h=h: scan(half("yb", h, 2), R("dbc"), half("sp", h, 2), A.mult, A.add),
+                "pw" + x: lambda h=h: turn(half("pw", h, 2), half("yb", h, 2)),
+                "pm" + x: lambda h=h: scan(half("pm", h, 2), R("alt"), half("pa", h, 2)),
+                "s1" + x: lambda h=h: scan(half("s1", 2 + h), half("dsel", 0), odd("pm", h)),
+                "s2" + x: lambda h=h: scan(half("s2", h), half("dsel", 0), half("z3", h)),
+                "s3" + x: lambda h=h: scan(half("s3", h), half("dsel", 0), half("rz", h)),
+                "lo" + x: lambda h=h, a=a, e=e: ts(R("plus", a, e, STEPS), last("s3", H * h, H), col("pf", 3), A.is_equal),
+                "kl" + x: lambda h=h, a=a, e=e: ts(R("plus", a + 1, e, STEPS), last("s3", H * h, H), col("lim", 1), A.is_ge),
+                "tf" + x: lambda a=a, e=e: scan(R("tf", a, e), R("times", a, e), R("plus", a, e), A.mult, A.add),
+                "tu" + x: lambda h=h, a=a, e=e: copy(R("tu", NK // 2 * h, NK // 2 * (h + 1)), R("tf", a + STEPS - 1, e, STEPS)),
+                "g0" + x: lambda h=h: tt(plane("gw", 0, H * h, H * h + H), moves(plane("tw", 0, 0, F), "tu", 0, h), half("tc", h), A.add),
                 "S2" + x: lambda h=h: act(half("c2", h), moves(R("pm"), "mo4", 0, h), ACT.Identity, 639.5, -4.0),
                 "V2" + x: lambda h=h: tt(odd("b2", h), moves(R("pm"), "mo3", 0, h), half("c2", h), A.is_ge),
                 "S3" + x: lambda h=h: act(half("ca", h), moves(R("b2"), "mo4", 0, h), scale=2.0),
@@ -496,7 +488,8 @@ def rank_program(g, core, T, topo):
         for w in ((FIRST if first else LATER) + REST).split():
             step[w]()
         for b in range(4):
-            tt(plane("gw", b), moves(plane("tw", b, 0, F), "tu", 0), R("tc", C * b, C * b + C), A.add)
+            if b > 0:
+                tt(plane("gw", b), moves(plane("tw", b, 0, F), "tu", 0), R("tc", C * b, C * b + C), A.add)
             if b < 3:
                 act(elems("zt", b), moves(plane("gw", b, 0, F), "tu", 0), scale=1.0 / 64)
         ts(elems("zt", 3, H, C), moves(plane("gw", 3, 0, F), "tu", 0, 1), 1.0 / 64, A.mult)

import numpy as np
from concourse.mybir import dt, AluOpType, AxisListType, ActivationFunctionType

C, K, ROUNDS = 448, 128, 3
F = C + K
H = C // 2
LAST = H
NK = C // 16
BIG = 2.0 ** 90
OFF = 1024.0
MID = 192.0
NS = 7
SUMS = (((7,), (4, 8, 5, 6), (13, 11, 9, 12, 10)), ((6, 7), (4, 8, 5), (13, 11, 9, 12, 10)))
NP = (NK - 1 - NS) // 2
WIDTH = [max(128, C - 64 * s) for s in range(7)]
START = [sum(WIDTH[:s]) for s in range(8)]
CODES, PLANE = "float8_e4m3fn_x4", "uint8"
STEPS = 7

FIRST = """sp pu yba ybb pwa pwb a0 a1 ow s0 osel pma ou pmb border S2a S2b pt dd s1a s1b t1 b3 wa f2 mo3 send V2a V2b
           S3a S3b nl np eq """
LATER = """sp pu pt dd nl np yba ybb pwa pwb a0 a1 ow s0 osel pma ou pmb border S2a S2b s1a s1b t1 b3 wa f2 mo3 send V2a V2b
           S3a S3b vq """
REST = "hh V3a V3b S4a S4b unpack s2a s2b V4a e1 V4b s3a e0 s3b loa kla lob klb tfa tfb tua tub g0a g0b"

BUFFERS = {
    "bfloat16": dict(xt=4 * C, ut=512, vt=512, ci=H, e0=K, e1=K, mask=H, dx=H, dsel=C, dbc=C, alt=C, gd=512,
                     bd=512, nil=516, et0=516, et1=516, ew=516, uu=4 * START[7], sg=3 * C, cj=C, sp=2 * C, yb=2 * C,
                     pw=2 * C, bt=4 * K, pa=2 * C, pm=2 * C + 16, c2=C, b2=2 * C + 16, ca=C, z3=C, r0=C, rz=C, tw=4 * F,
                     tc=4 * C, gw=4 * F, zt=4 * C),
    "float32": dict(w0=2 * NK, w1=2 * NK, wa=2 * NK, pf=12, k4=4, lim=4, kc=4, off=4, num=F, mk=C, sc=C, acc=NS + NP, a2w=NK, pl=NK,
                    junk=192 * NP, dd=NK, ow=C, osel=K, t0=2 * NK, otr=C, ya=C - LAST, yc=LAST,
                    csel=C, times=STEPS * NK, plus=STEPS * NK, tf=STEPS * NK),
    "float16": dict(rd=C, s1=2 * C, s2=C, s3=C),
    "int32": dict(uoi=8, mvt=2 * NK, mi=2 * NK, pi=4, rr=NK + NP),
    "uint16": dict(uo=8, mo=2 * NK, mo2=2 * NK, mo3=NK, mo4=NK, pu=NK, ou=8, tu=NK),
    CODES: dict(xq=C, uq0=128, uq=128, vq=128, wq=512, bq=384, eq=512, cq=START[7], zq=C, sq0=K, sq1=K, sq2=K, lq0=K, lq1=K, lq2=K),
    PLANE: dict(xs=C, us0=128, us=128, vs=128, wp=512, bs=384, es=512, cs=START[7], zs=C, ss0=K, ss1=K, ss2=K, ls0=K, ls1=K, ls2=K),
}
SCRATCH = {name: ("sbuf", [128, n], kind) for kind in BUFFERS for name, n in BUFFERS[kind].items()}
SCRATCH.update({"p%d" % b: ("psum", [128, 512], "float32") for b in range(8)})

SEMAPHORES = ["cv", "ca", "ct", "cg", "lx", "lx2", "lu", "lm", "lw", "lp", "lv", "sent", "arr0", "arr1", "arr2",
              "z0", "z1", "z2", "z3", "y4", "y5", "y6", "tw0", "tw1", "tw2", "tw3", "o1", "o2", "o3", "o4", "o5", "o6"]

A = AluOpType
ACT = ActivationFunctionType


def rank_program(g, core, T, topo):
    rank = T.rank_of(core)
    if rank is None:
        return
    n_ranks = len(T.cores)
    dst = T.cores[(rank - 1) % n_ranks]
    src_core = T.cores[(rank + 1) % n_ranks]
    queue = {"v": g.vector, "s": g.scalar, "t": g.tensor, "g": g, "y": g.sync}
    own = {"v": "cv", "s": "ca", "t": "ct", "g": "cg"}
    count = {s: 0 for s in SEMAPHORES}
    seen = {q: {s: 0 for s in SEMAPHORES} for q in queue}
    wrote = {b: {} for b in SCRATCH}
    read = {b: {} for b in SCRATCH}

    def R(name, a=0, b=None, step=1):
        return (name, a, SCRATCH[name][1][1] if b is None else b, step)

    def ap(r):
        if isinstance(r, tuple):
            if len(r) == 2:
                return ap(r[0]).indirect(ap(r[1]))
            return T[r[0]][:, r[1]:r[2]] if r[3] == 1 else T[r[0]][:, r[1]:r[2]:r[3]]
        return r

    def raw(r):
        return ap(r).bitcast(dt.uint8) if SCRATCH[r[0]][2] == CODES else ap(r)

    def parts(rs):
        out = []
        for r in rs:
            if isinstance(r, tuple):
                out += list(r) if len(r) == 2 else [r]
        return out

    def span(r):
        return slice(None) if SCRATCH[r[0]][0] == "psum" else slice(r[1], r[2], r[3])

    def wait(q, sem, val):
        if val > seen[q][sem]:
            queue[q].wait_ge(T.sem[sem], val)
            seen[q][sem] = val

    def mark(table, r, sem, val):
        if sem not in table[r[0]]:
            table[r[0]][sem] = np.zeros(SCRATCH[r[0]][1][1], np.int64)
        table[r[0]][sem][span(r)] = val

    def before(q, reads, writes):
        need = {}
        for r, w in [(r, False) for r in reads] + [(r, True) for r in writes]:
            bank = SCRATCH[r[0]][0] == "psum"
            for table, use in ((wrote, True), (read, w or bank)):
                for sem, v in table[r[0]].items():
                    if not use or (bank and sem == own.get(q) and (q == "t" or table is read)):
                        continue
                    need[sem] = max(need.get(sem, 0), int(v[span(r)].max()))
        for sem in need:
            wait(q, sem, need[sem])

    def op(q, make, reads, writes, sem=None, inc=1):
        reads, writes, sem = parts(reads), parts(writes), sem or own[q]
        before(q, reads, writes)
        count[sem] += inc
        make().then_inc(T.sem[sem], inc)
        for r in reads:
            mark(read, r, sem, count[sem])
        for r in writes:
            mark(wrote, r, sem, count[sem])

    V, S, PE = g.vector, g.scalar, g.tensor

    def copy(out, in_):
        op("v", lambda: V.tensor_copy(ap(out), ap(in_)), [in_], [out])

    def tt(out, a, b, f):
        op("v", lambda: V.tensor_tensor(ap(out), ap(a), ap(b), f), [a, b], [out])

    def ts(out, a, s1, f1, s2=None, f2=None):
        if f2 is None:
            op("v", lambda: V.tensor_scalar(ap(out), ap(a), ap(s1), None, f1), [a, s1], [out])
        else:
            op("v", lambda: V.tensor_scalar(ap(out), ap(a), ap(s1), ap(s2), f1, f2), [a, s1, s2], [out])

    def scan(out, d0, d1, f0=A.add, f1=A.max):
        op("v", lambda: V.tensor_tensor_scan(ap(out), ap(d0), ap(d1), 0.0, f0, f1), [d0, d1], [out])

    def total(out, in_):
        op("v", lambda: V.tensor_reduce(ap(out), ap(in_), AxisListType.X, A.add), [in_], [out])

    def turn(out, in_):
        op("v", lambda: V.transpose(ap(out), ap(in_)), [in_], [out])

    def fill(out, val):
        op("v", lambda: V.memset(ap(out), val), [], [out])

    def quant(q, s, in_):
        op("v", lambda: V.quantize_mx(ap(q), ap(s), ap(in_)), [in_], [q, s])

    def act(out, in_, func=ACT.Copy, bias=None, scale=1.0, acc=None):
        kw = {"scale": ap(scale)}
        if bias is not None:
            kw["bias"] = ap(bias)
        if acc is not None:
            kw["accum_out"] = ap(acc)
        op("s", lambda: S.activation(ap(out), ap(in_), func, **kw), [in_, bias, scale], [out, acc])

    def mm(out, wq, wsc, xq, xsc, start=True, stop=True):
        op("t", lambda: PE.matmul_mx(ap(out), ap(wq), ap(wsc), ap(xq), ap(xsc), start, stop), [wq, wsc, xq, xsc], [out])

    def iota(out, pattern, base=0, mult=0):
        kw = {} if SCRATCH[out[0]][2] == "int32" else {"allow_small_or_imprecise_dtypes": True}
        op("g", lambda: g.iota(ap(out), pattern, base, mult, **kw), [], [out])

    def where(out, in_, pattern, f, other, base, mult):
        op("g", lambda: g.affine_select(ap(out), ap(in_), pattern, f, other, base, mult), [in_], [out])

    def load(q, out, src, sem):
        op(q, lambda: queue[q].dma_start(raw(out), src), [], [out], sem, 16)

    def store(q, to, src, r, sem):
        op(q, lambda: queue[q].dma_start(to, src), [r], [], sem, 16)

    def col(name, j):
        return R(name, j, j + 1)

    def last(name, a=0, n=C):
        return R(name, a + 15, a + n, 16)

    def plane(name, b, a=0, e=C):
        return R(name, F * b + a, F * b + e)

    def elems(name, b, a=0, e=C):
        return R(name, 4 * a + b, 4 * e, 4)

    def block(name, b):
        return R(name, 128 * b, 128 * b + 128)

    def half(name, h, w=1):
        return R(name, w * H * h, w * H * (h + 1))

    def bank(b, n, a=0):
        return R("p%d" % b, a, n)

    def times(j):
        return R("times", j, STEPS * NK, STEPS)

    def plus(j):
        return R("plus", j, STEPS * NK, STEPS)

    load("s", R("ut"), T.u[:], "lu")
    load("y", half("xt", 1, 4), T.x[:, 2 * C:4 * C], "lx")
    load("y", half("xt", 0, 4), T.x[:, 0:2 * C], "lx2")
    load("s", R("mvt"), T.mv[:], "lm")
    before("y", [R("xt")], [])

    iota(col("pi", 0), [[0, 1]], 0, 1)
    iota(R("uoi"), [[16, 8]])
    iota(R("ci", 0, K + 16), [[0, K // 16 + 1], [1, 16]])
    iota(R("ci", K + 16, H), [[0, (H - K) // 16 - 1], [1, 16]])
    iota(R("k4"), [[127, 2], [35, 2]], 1)
    iota(R("kc"), [[320, 2], [192, 2]], 15 - int(MID))
    fill(R("nil"), 0.0)
    where(R("dx"), R("nil", 0, H), [[0, NK // 2], [1, 16]], A.not_equal, -32 * BIG, 0, 0)
    where(R("et0"), R("nil"), [[1, 516]], A.not_equal, 1.0, -2, -4)
    where(R("ew"), R("et0"), [[1, 516]], A.not_equal, 512.0, -3, -4)
    where(R("gd"), R("nil", 0, 512), [[16, 8], [0, 64]], A.is_gt, 1.0, 0, -1)
    where(R("bd"), R("gd"), [[16, 8], [0, 64]], A.is_ge, 0.0, 15, -1)
    iota(R("cj"), [[-16, NK], [1024, 16]])
    iota(col("rr", 0), [[0, 1]])
    where(half("dbc", 0, 2), R("nil", 0, C), [[0, NK // 2], [1, 32]], A.is_equal, 1.0, 0, 0)
    where(R("times"), R("nil", 0, STEPS * NK), [[0, NK], [1, STEPS]], A.is_equal, 1.0, 0, 0)
    iota(R("num"), [[1, F]])
    iota(half("alt", 0, 2), [[0, H], [4096, 2]], -4096)
    iota(R("w0"), [[0, NK], [1024, 2]])
    iota(R("pm", 2 * C, 2 * C + 16), [[0, 16]], -200)
    iota(R("b2", 2 * C, 2 * C + 16), [[0, 16]], -8)
    where(R("et1"), R("nil"), [[1, 516]], A.not_equal, 1.0, -3, -4)

    def move(to, src, sem):
        op("y", lambda: g.sync.dma_start(ap(to), ap(src)), [src], [to], sem, 16)

    def pad(s):
        to = R("uu", 4 * (START[s] + C - 64 * s - 48), 4 * START[s + 1])
        if s < 4:
            act(to, R("nil", 0, to[2] - to[1]))
        else:
            move(to, R("nil", 0, to[2] - to[1]), "y%d" % s)

    ts(col("pi", 1), col("pi", 0), 15, A.bitwise_and)
    ts(col("pi", 3), col("pi", 0), 16, A.bitwise_and)
    copy(R("uo"), R("uoi"))
    copy(R("pf", 0, 3, 2), R("pi", 1, 4, 2))
    ts(col("pf", 8), col("pi", 1), -BIG, A.mult)
    ts(col("pf", 3), col("pi", 1), 15.0, A.is_lt, OFF, A.mult)
    for s in (2, 3, 0):
        pad(s)
    act(R("mask"), R("ci"), ACT.Abs, col("pf", 8), BIG)
    pad(1)
    ts(R("e0"), R("ci", 0, K), col("pf", 0), A.is_equal, -4 * OFF, A.mult)
    ts(R("e1"), R("ci", 15, K + 15), col("pf", 0), A.is_equal, OFF, A.mult)
    tt(R("dsel", 0, K), R("e0"), R("e1"), A.add)
    ts(R("mi"), R("mvt"), 512 - 16, A.bitwise_and)
    copy(R("mo"), R("mvt"))
    ts(R("lim"), R("k4"), col("pf", 3), A.add)
    tt(R("t0"), R("mi"), R("mvt"), A.add)
    quant(R("uq0"), R("us0"), R("ut"))
    ts(R("off"), R("kc"), col("pf", 3), A.subtract, col("pf", 0), A.subtract)
    op("v", lambda: V.tensor_copy(ap(R("uq")).bitcast(dt.uint32), ap(R("uq0")).bitcast(dt.uint32).indirect(ap(R("uo")))),
       [R("uq0"), R("uo")], [R("uq")])
    op("s", lambda: S.activation(ap(R("us")), ap((R("us0"), R("uo"))), ACT.Copy), [R("us0"), R("uo")], [R("us")])
    for b in range(2):
        act(plane("tw", b, H, C), elems("xt", b, H, C), scale=32.0)

    for s in (4, 5, 6):
        pad(s)
    load("y", R("wq"), T.wc[:], "lw")
    load("y", R("wp"), T.ws[:], "lp")
    load("y", R("vt"), T.v[:], "lv")
    move(R("dsel", K, 2 * K), R("dsel", 0, K), "z0")
    move(R("dsel", 2 * K, C), R("dsel", 0, C - 2 * K), "z1")
    for name, sem in (("sp", "z2"), ("b2", "z3")):
        for j in range(2):
            move(half(name, j, 2), R("nil", 0, C), sem)
        mark(wrote, R(name, 0, 2 * C), sem, count[sem])


    def slot(sg, a, b):
        at = START[sg // 4]
        return R("uu", 4 * (at + a) + sg % 4, 4 * (at + b), 4)

    def qtiles(s, w):
        a = START[s]
        quant(R("cq", a, a + w), R("cs", a, a + w), R("uu", 4 * a, 4 * (a + w)))

    def mcount(b, j, a, w, start=True, stop=True):
        mm(bank(b, w), block("bq", j), block("bs", j), R("cq", a, a + w), R("cs", a, a + w), start, stop)

    def mtile(s, start=False, stop=False):
        mcount(3, 0, START[s], WIDTH[s], start, stop)

    def mpair(q, b, runs):
        s = q // 2
        w = WIDTH[s] // runs
        for j in range(runs):
            mcount(b, 1 + q % 2, START[s] + w * j, w, j == 0, j == runs - 1)

    def spair(q, who):
        b, a, w = (q, 0, WIDTH[q // 2] // 2) if q < 8 else (q % 2, START[q // 2] - START[4], C - 32 * q)
        to = col("acc", NS + 13 - q)
        if who == "s":
            act(R("junk", 192 * (13 - q), 192 * (13 - q) + w), bank(b, a + w, a), acc=to)
        else:
            total(to, bank(b, a + w, a))

    def sign(sg):
        a = C - 16 * sg
        act(R("sg", sg % 3 * C, sg % 3 * C + a), bank(2, a), ACT.Sign, col("sc", a + 15), -1.0)

    def relu(sg):
        a = C - 16 * sg
        act(slot(sg, 0, a), R("sg", sg % 3 * C, sg % 3 * C + a), ACT.Relu, acc=col("acc", NS - sg))

    def rows(first, end):
        for sg in range(first, end):
            a = C - 16 * sg
            ts(slot(sg, 0, a), bank(1, a), col("sc", a + 15), A.is_lt)

    def qstate(a, e):
        quant(R("xq", a, e), R("xs", a, e), R("xt", 4 * a, 4 * e))

    def upper_scores():
        mm(bank(0, H), R("uq"), R("us"), half("xq", 1), half("xs", 1))

    def moves(win, lst, k, h=None):
        a, e = (0, NK) if h is None else (NK // 2 * h, NK // 2 * (h + 1))
        return (win, R(lst, NK * k + a, NK * k + e))

    def twin(b):
        move(R("tc", C * b, C * b + C), plane("tw", b), "tw%d" % b)

    m0, m1, p128 = R("mvt", 0, NK), R("mvt", NK, 2 * NK), plus(6)

    for n in range(ROUNDS):
        first, final = n == 0, n == ROUNDS - 1
        if first:
            qstate(H, C)
            upper_scores()
            ts(R("mo2"), R("t0"), col("pf", 2), A.add)
            qstate(0, H)
        for b, w in ((1, WIDTH[2]), (2, C)):
            mm(bank(b, w), R("uq"), R("us"), R("xq", 0, w), R("xs", 0, w))
        tt(half("mk", 1), bank(0, H), R("mask"), A.subtract)
        if first:
            ts(R("w1", 1, 2 * NK, 2), m1, 2.0, A.mult, 1.0, A.add)
        scan(half("sc", 1), R("dx"), half("mk", 1))
        tt(half("mk", 0), bank(1, H), R("mask"), A.subtract)
        sign(1)
        sign(2)
        relu(1)
        sign(3)
        relu(2)
        sign(4)
        relu(3)
        rows(8, 10)
        scan(half("sc", 0), R("dx"), half("mk", 0))
        rows(10, 13)
        if first:
            for j in range(2):
                quant(block("bq", 1 + j), block("bs", 1 + j), R("ew", 2 - 2 * j, 514 - 2 * j))
        qtiles(2, WIDTH[2])
        mpair(4, 4, 2)
        mpair(5, 5, 2)
        rows(13, 17)
        qtiles(3, WIDTH[3])
        mpair(6, 6, 2)
        mpair(7, 7, 2)
        sign(5)
        relu(4)
        for h in range(2):
            tt(slot(0, H * h, H * h + H), bank(1 - h, H), half("sc", h), A.is_le)
        rows(17, 18)
        if first:
            quant(block("bq", 0), block("bs", 0), R("bd"))
        qtiles(0, C)
        for s in (0, 2, 3):
            mtile(s, start=s == 0)
        rows(18, 28)
        scan(R("rd"), R("cj"), slot(0, 0, C), A.min, A.add)
        qtiles(4, 448 if first else 384)
        for j in range(2):
            mcount(j, 1 + j, START[4], 384)
        for s in (4, 5, 6):
            mtile(s)
        sign(6)
        relu(5)
        sign(7)
        relu(6)
        relu(7)
        if first:
            ts(R("mo4"), m0, 2.0, A.mult, 1.0, A.add)
        early, by_s, late = SUMS[min(n, 1)]
        for q in early:
            spair(q, "v")
        qtiles(1, WIDTH[1])
        mtile(1, stop=True)
        for q in by_s:
            spair(q, "s")
        for q in late:
            spair(q, "v")
        copy(R("rr", NK - NS, NK + NP), R("acc"))
        scan(R("csel"), R("dsel", 0, C), bank(3, C))
        ts(R("rr", 2, 2 * NP + 1, 2), R("rr", NK, NK + NP), 511, A.bitwise_and)
        ts(R("rr", 1, 2 * NP + 1, 2), R("rr", NK, NK + NP), 9, A.logical_shift_right)
        tt(R("a2w"), last("csel"), last("rd"), A.subtract)
        if first:
            for b in range(4):
                e = H if b < 2 else C
                act(plane("tw", b, 0, e), elems("xt", b, 0, e), scale=32.0)
                twin(b)
        tt(R("pl"), R("a2w"), R("rr", 0, NK), A.subtract)
        sq, ss, lq, ls, arr = R("sq%d" % n), R("ss%d" % n), R("lq%d" % n), R("ls%d" % n), "arr%d" % n

        def border():
            for b in range(3):
                act(elems("bt", b, 0, K), (plane("tw", b), R("ou")), scale=1.0 / 32)

        def send():
            quant(sq, ss, R("bt"))
            before("g", [sq, ss], [])
            rid, pid = topo.addr(dst)[0:2]
            for to, src in ((lq, sq), (ls, ss)):
                g.remote_dma(raw(to), raw(src), T.sem[arr], T.sem["sent"], pid, rid, topo.mask(core, dst))
                count["sent"] += len(topo.engines(core, dst))
                count[arr] += len(topo.engines(src_core, core))
            mark(wrote, lq, arr, count[arr])
            mark(wrote, ls, arr, count[arr])

        def unpack():
            for b in range(4):
                mm(bank(b, K), block("eq", b), block("es", b), lq, ls)
            for name, scale in (("tw", 32.0), ("gw", 64.0)):
                for b in range(4):
                    act(plane(name, b, C, F), bank(b, K), scale=scale)

        def unpackers():
            for b in range(4 * first):
                a = 2 - 2 * (b // 2)
                quant(block("eq", b), block("es", b), R("et%d" % (b % 2), a, a + 512))
            if first:
                tt(times(4), m1, m0, A.subtract)
                copy(plus(4), m0)

        def odd(name, h):
            return R(name, C * h + 1, C * h + C, 2)

        step = dict(
            sp=lambda: ts(R("sp", 0, 2 * C, 32), R("pl"), col("off", 0), A.add, 128.0, A.min),
            pu=lambda: ts(R("pu"), R("pl"), col("off", 1), A.add),
            pt=lambda: act(p128, R("pl"), ACT.Identity, col("off", 2)),
            ow=lambda: op("v", lambda: V.tensor_copy(ap((R("ow"), R("pu"))), ap(R("num", 0, C))), [R("num", 0, C), R("pu")], [R("ow")]),
            osel=lambda: scan(R("osel"), R("dsel", 0, K), R("ow", 0, K)),
            ou=lambda: ts(R("ou"), last("osel", 0, K), col("pf", 3), A.subtract),
            b3=lambda: ts(elems("bt", 3, 0, K), (plane("tw", 3), R("ou")), 1.0 / 32, A.mult),
            border=border, send=send, unpack=unpack, eq=unpackers,
            vq=lambda: quant(R("vq"), R("vs"), R("vt")) if n == 1 else None,
            dd=lambda: act(R("dd"), p128, ACT.Relu, -2048.0 * (C - 0.5), 2048.0),
            nl=lambda: act(times(6), R("dd"), ACT.Relu, 1.0, -1.0),
            np=lambda: act(plus(5), p128, scale=-1.0),
            a0=lambda: act(R("pa", 0, 2 * C, 2), moves(R("pw"), "mo2", 0)),
            a1=lambda: act(R("pa", 1, 2 * C, 2), moves(R("pw"), "mo2", 1)),
            s0=lambda: scan(R("s1", 0, C), R("dsel"), R("pa", 0, 2 * C, 2)),
            t1=lambda: ts(R("w1", 0, 2 * NK, 2), last("s1", C), col("lim", 2), A.is_ge),
            wa=lambda: scan(R("wa"), R("w0"), R("w1"), A.mult, A.add),
            mo3=lambda: ts(R("mo3"), R("wa", 1, 2 * NK, 2), 2.0 * C, A.min),
            f2=lambda: tt(times(1), last("s1"), last("s1", C), A.is_equal),
            hh=lambda: tt(plus(2), R("w1", 0, 2 * NK, 2), times(1), A.is_gt),
            e1=lambda: ts(plus(3), last("s2"), col("lim", 0), A.is_equal),
            e0=lambda: ts(times(2), last("s2"), col("pf", 3), A.is_equal))
        for h, x in enumerate("ab"):
            a, e = STEPS * NK // 2 * h, STEPS * NK // 2 * (h + 1)
            step.update({
                "yb" + x: lambda h=h: scan(half("yb", h, 2), R("dbc"), half("sp", h, 2), A.mult, A.add),
                "pw" + x: lambda h=h: turn(half("pw", h, 2), half("yb", h, 2)),
                "pm" + x: lambda h=h: scan(half("pm", h, 2), R("alt"), half("pa", h, 2)),
                "s1" + x: lambda h=h: scan(half("s1", 2 + h), half("dsel", 0), odd("pm", h)),
                "s2" + x: lambda h=h: scan(half("s2", h), half("dsel", 0), half("z3", h)),
                "s3" + x: lambda h=h: scan(half("s3", h), half("dsel", 0), half("rz", h)),
                "lo" + x: lambda h=h, a=a, e=e: ts(R("plus", a, e, STEPS), last("s3", H * h, H), col("pf", 3), A.is_equal),
                "kl" + x: lambda h=h, a=a, e=e: ts(R("plus", a + 1, e, STEPS), last("s3", H * h, H), col("lim", 1), A.is_ge),
                "tf" + x: lambda a=a, e=e: scan(R("tf", a, e), R("times", a, e), R("plus", a, e), A.mult, A.add),
                "tu" + x: lambda h=h, a=a, e=e: copy(R("tu", NK // 2 * h, NK // 2 * (h + 1)), R("tf", a + STEPS - 1, e, STEPS)),
                "g0" + x: lambda h=h: tt(plane("gw", 0, H * h, H * h + H), moves(plane("tw", 0, 0, F), "tu", 0, h), half("tc", h), A.add),
                "S2" + x: lambda h=h: act(half("c2", h), moves(R("pm"), "mo4", 0, h), ACT.Identity, 639.5, -4.0),
                "V2" + x: lambda h=h: tt(odd("b2", h), moves(R("pm"), "mo3", 0, h), half("c2", h), A.is_ge),
                "S3" + x: lambda h=h: act(half("ca", h), moves(R("b2"), "mo4", 0, h), scale=2.0),
                "V3" + x: lambda h=h: tt(half("z3", h), moves(R("b2"), "mo3", 0, h), half("ca", h), A.add),
                "S4" + x: lambda h=h: act(half("r0", h), moves(R("z3"), "mo", 0, h), ACT.Square),
                "V4" + x: lambda h=h: tt(half("rz", h), moves(R("z3"), "mo", 1, h), half("r0", h), A.mult)})
        for w in ((FIRST if first else LATER) + REST).split():
            step[w]()
        for b in range(4):
            if b > 0:
                tt(plane("gw", b), moves(plane("tw", b, 0, F), "tu", 0), R("tc", C * b, C * b + C), A.add)
            if b < 3:
                act(elems("zt", b), moves(plane("gw", b, 0, F), "tu", 0), scale=1.0 / 64)
        ts(elems("zt", 3, H, C), moves(plane("gw", 3, 0, F), "tu", 0, 1), 1.0 / 64, A.mult)
        act(elems("zt", 3, 0, H), moves(plane("gw", 3, 0, F), "tu", 0, 0), scale=1.0 / 64)
        if final:
            act(R("otr"), moves(R("num"), "tu", 0))
            store("y", T.ot[:], T.otr[0:128:16, :], R("otr"), "o1")
        cut = LAST if final else H
        for h, a, e in ((1, cut, C), (0, 0, cut)):
            quant(R("zq", a, e), R("zs", a, e), R("zt", 4 * a, 4 * e))
            for b in range(4):
                mm(bank(4 - 4 * h + b, e - a), block("wq", b), block("wp", b), R("zq", a, e), R("zs", a, e))
        for h, a, e in ((1, cut, C), (0, 0, cut)):
            for b in range(4):
                tt(plane("tw", b, a, e), plane("tw", b, a, e), bank(4 - 4 * h + b, e - a), A.add)
                if h == 1 or b < 2:
                    act(elems("xt", b, a, e), plane("tw", b, a, e), scale=1.0 / 32)
                if h == 0 and not final:
                    twin(b)
        qstate(cut, C)
        if final:
            mm(bank(0, C - cut), R("vq"), R("vs"), R("xq", cut), R("xs", cut))
            store("y", T.oc[:, 4 * cut:4 * C], raw(R("xq", cut)), R("xq", cut), "o2")
            act(R("ya"), bank(0, C - cut))
            store("s", T.y[:, cut:C], ap(R("ya")), R("ya"), "o4")
        else:
            upper_scores()
        for b in (2, 3):
            ts(elems("xt", b, 0, cut), plane("tw", b, 0, cut), 1.0 / 32, A.mult)
        qstate(0, cut)

    mm(bank(1, LAST), R("vq"), R("vs"), R("xq", 0, LAST), R("xs", 0, LAST))
    store("s", T.oc[:, 0:4 * LAST], raw(R("xq", 0, LAST)), R("xq", 0, LAST), "o6")
    for k in range(4):
        store("sy"[k % 2], T.osc[4 * k:4 * k + 4, :], T.xs[32 * k:32 * k + 4, :], R("xs"), "o3")
    copy(R("yc"), bank(1, LAST))
    store("y", T.y[:, 0:LAST], ap(R("yc")), R("yc"), "o5")
    for sem in SEMAPHORES:
        if max(seen[q][sem] for q in queue) < count[sem]:
            wait("g", sem, count[sem])
